import numpy as np
import ml_dtypes


def mxq(x, axis, fmt="e4m3"):
    dtype, down = {"e4m3": (ml_dtypes.float8_e4m3fn, 7), "e5m2": (ml_dtypes.float8_e5m2, 14)}[fmt]
    v = np.moveaxis(np.asarray(x, np.float32).astype(ml_dtypes.bfloat16).astype(np.float64), axis, -1)
    blocks = v.reshape(v.shape[:-1] + (-1, 32))
    amax = np.abs(blocks).max(-1, keepdims=True)
    byte = np.maximum(np.where(amax > 0, np.frexp(amax)[1] - 1 + 127, 0) - down, 1)
    scale = np.exp2(byte - 127.0)
    codes = (blocks / scale).astype(np.float32).astype(dtype).astype(np.float64)
    return np.moveaxis((codes * scale).reshape(v.shape), -1, axis)


WIDE = False


def mx_kscale(k):
    if not WIDE:
        return np.ones(k)
    levels = np.array([10, -10, 5, -5, 0])
    if k % 512:
        return np.exp2(np.random.permutation(np.resize(levels, k // 32))).repeat(32)
    a = np.empty((k // 512, 16))
    for p in range(k // 512):
        a[p, :8] = np.random.permutation(np.resize(levels, 8))
        for g in range(8):
            far = levels[np.abs(levels - a[p, g]) >= 10]
            a[p, g + 8] = far[np.random.randint(len(far))]
    return np.exp2(a.ravel()).repeat(32)


def f64(x):
    return np.asarray(x).astype(np.float64)


def striped(idx):
    return np.tile(idx.reshape(-1, 16).T, (8, 1)).astype(np.uint16)


def unstriped(offs):
    return offs[:16].T.reshape(-1).astype(np.int64)


K, T, D, S, V, N = 1536, 1024, 4, 512, 256, 512


def setup_inputs():
    n = np.random.standard_normal
    s = mx_kscale(K)[:, None]
    return {
        "xT": (n((K, T)) * s).astype(np.float32),
        "w": (n((K, N)) / np.sqrt(K) / s).astype(np.float32),
        "b": (0.3 * n((N, 1))).astype(np.float32),
        "gate": np.tile(np.random.uniform(0.2, 1.0, (D, 1, V)) / np.sqrt(D), (1, N, 1)).astype(np.float32),
        "offs": striped(np.random.permutation(T)[:S]),
        "pos1": striped(np.random.permutation(S)[:V]),
        "pos2": striped(np.random.permutation(S)[:V]),
        "pos3": striped(np.random.permutation(S)[:V]),
        "pos4": striped(np.random.permutation(S)[:V]),
    }


def reference(xT, w, b, gate, offs, pos1, pos2, pos3, pos4):
    idx = unstriped(offs)
    xq = mxq(f64(xT)[:, idx], 0, "e4m3")
    y = mxq(f64(w), 0, "e4m3").T @ xq
    y = y + f64(b)
    return sum(f64(gate[d]) * y[:, unstriped(p)] for d, p in enumerate((pos1, pos2, pos3, pos4)))

@@ -1,0 +1,229 @@
+from contextlib import ExitStack
+
+import concourse.mybir as mybir
+from concourse.masks import make_identity
+
+K, T, D, S, V, N = 1536, 1024, 4, 512, 256, 512
+FLOPS = 2 * K * N * S
+
+F32 = mybir.dt.float32
+BF16 = mybir.dt.bfloat16
+U32 = mybir.dt.uint32
+U16 = mybir.dt.uint16
+U8 = mybir.dt.uint8
+FP8X4 = mybir.dt.float8_e4m3fn_x4
+ACT = mybir.ActivationFunctionType
+ALU = mybir.AluOpType
+
+P = 128
+PACK = 4
+K_PASS = P * PACK
+PASSES = K // K_PASS
+BLOCKS = N // P
+RUN = 4
+
+X_CHUNKS = [
+    (0, 0, 256, 96), (0, 256, 256, 96), (0, 512, 512, 160),
+    (1, 0, 512, 160), (1, 512, 512, 160),
+    (2, 0, 256, 96), (2, 256, 256, 96), (2, 512, 256, 112), (2, 768, 128, 64), (2, 896, 128, 80),
+]
+PE_SUM_BLOCKS = 3
+
+
+def interleave_views(raw, grouped, lo, hi):
+    src = raw[:, :, lo:hi].rearrange("p j (c i) -> p c j i", i=RUN)
+    dst = grouped[:, lo:hi, :].rearrange("p (c i) j -> p c j i", i=RUN)
+    return dst, src
+
+
+def tile_picked_sub_lin_bias_sub_e_kernel(tc, xT, w, b, gate, offs, pos1, pos2, pos3, pos4, out):
+    nc = tc.nc
+    with ExitStack() as ctx:
+        keep = ctx.enter_context(tc.tile_pool(name="keep", bufs=1))
+        psum = ctx.enter_context(tc.psum_pool(name="psum", bufs=2))
+
+        picked = keep.tile([P, S // 16], U16, name="picked")
+        neigh = [keep.tile([P, V // 16], U16, name=f"neigh{d}") for d in range(D)]
+        bias = keep.tile([P, BLOCKS], F32, name="bias")
+        x_raw = [keep.tile([P, PACK, n], F32, name=f"x_raw{c}") for c, (a, t0, n, nv) in enumerate(X_CHUNKS)]
+        x_bf = [keep.tile([P, n, PACK], BF16, name=f"x_bf{c}", align_bytes=64) for c, (a, t0, n, nv) in enumerate(X_CHUNKS)]
+        x_words = [keep.tile([P, T], U32, name=f"x_words{a}", align_bytes=64) for a in range(PASSES)]
+        x_bytes = keep.tile([P, T], U8, name="x_bytes", align_bytes=64)
+        got_words = {}
+        got_bytes = keep.tile([P, S], U8, name="got_bytes", align_bytes=64)
+        w_raw = [[keep.tile([P, PACK, P], F32, name=f"w_raw{m}_{a}", tag=f"w_raw{m}_{a}") for a in range(PASSES)] for m in range(BLOCKS)]
+        w_bf = [keep.tile([P, PASSES, P, PACK], BF16, name=f"w_bf{m}", tag=f"w_bf{m}", align_bytes=64) for m in range(BLOCKS)]
+        w_words = [keep.tile([P, PASSES, P], U32, name=f"w_words{m}", align_bytes=64) for m in range(BLOCKS)]
+        w_bytes = [keep.tile([P, PASSES, P], U8, name=f"w_bytes{m}", align_bytes=64) for m in range(BLOCKS)]
+        gates = [keep.tile([P, D, V], F32, name=f"gates{m}") for m in range(BLOCKS)]
+        y = {}
+        terms = {}
+        bias_rows = keep.tile([P, P], F32, name="bias_rows")
+        turned = [keep.tile([P, V], F32, name=f"turned{m}") for m in range(BLOCKS)]
+        result = [keep.tile([P, V], F32, name=f"result{m}") for m in range(BLOCKS)]
+        ident = keep.tile([P, P], F32, name="ident")
+        warm = keep.tile([P, 8], F32, name="warm")
+        warm2 = keep.tile([P, 8], F32, name="warm2")
+
+        def load_x(c):
+            a, t0, n, nv = X_CHUNKS[c]
+            rows = xT[a * K_PASS : (a + 1) * K_PASS, t0 : t0 + n]
+            nc.sync.dma_start(out=x_raw[c][:], in_=rows.rearrange("(p j) t -> p j t", j=PACK))
+
+        def load_w(m, a):
+            rows = w[a * K_PASS : (a + 1) * K_PASS, m * P : (m + 1) * P]
+            nc.sync.dma_start(out=w_raw[m][a][:], in_=rows.rearrange("(p j) n -> p j n", j=PACK))
+
+        def load_gate(m):
+            nc.sync.dma_start(out=gates[m][:], in_=gate[:, m * P : (m + 1) * P, :].rearrange("d p v -> p d v"))
+
+        nc.vector.memset(bias_rows[:], 0.0)
+        nc.scalar.dma_start(out=bias_rows[0:BLOCKS, :], in_=b.rearrange("(m p) o -> m (p o)", p=P))
+        load_x(0)
+        load_x(1)
+        nc.sync.dma_start(picked[:], offs)
+        for c in range(2, len(X_CHUNKS)):
+            load_x(c)
+        for a in range(PASSES):
+            load_w(0, a)
+        lists = (pos1, pos2, pos3, pos4)
+        nc.sync.dma_start(neigh[0][:], lists[0])
+        for a in range(PASSES):
+            load_w(1, a)
+            nc.sync.dma_start(neigh[a + 1][:], lists[a + 1])
+        for m in range(BLOCKS):
+            load_gate(m)
+            if m + 2 < BLOCKS:
+                for a in range(PASSES):
+                    load_w(m + 2, a)
+
+        nc.vector.memset(warm[:], 0.0)
+        nc.scalar.activation(warm2[:], warm[:], ACT.Identity)
+        nc.gpsimd.memset(x_bytes[:], 0)
+        make_identity(nc, ident[:])
+        bias_cols = psum.tile([P, P], F32, name="bias_cols", tag="back")
+        nc.tensor.transpose(bias_cols[:], bias_rows[:], ident[:])
+        nc.vector.tensor_copy(bias[:], bias_cols[:, 0:BLOCKS])
+
+        def cast_x(c):
+            a, t0, n, nv = X_CHUNKS[c]
+            dst, src = interleave_views(x_raw[c], x_bf[c], nv, n)
+            nc.scalar.activation(dst, src, ACT.Copy)
+            dst, src = interleave_views(x_raw[c], x_bf[c], 0, nv)
+            nc.vector.tensor_copy(dst, src)
+
+        def quantize_x(c):
+            a, t0, n, nv = X_CHUNKS[c]
+            nc.vector.quantize_mx(
+                out=x_words[a][:, t0 : t0 + n].bitcast(FP8X4),
+                scales=x_bytes[PACK * a :, t0 : t0 + n],
+                in_=x_bf[c][:].rearrange("p t j -> p (t j)"),
+            )
+
+        def gather_words(a):
+            got_words[a] = keep.tile([P, S], U32, name=f"got_words{a}", tag="w_bf0" if a == PASSES - 1 else f"got_words{a}", align_bytes=64)
+            parts = 2 if a == PASSES - 1 else 1
+            for h in range(parts):
+                n = S // parts
+                nc.vector.tensor_copy(got_words[a][:, h * n : (h + 1) * n], x_words[a][:].indirect(picked[:, h * n // 16 : (h + 1) * n // 16]))
+
+        def cast_w(m, a):
+            dst, src = interleave_views(w_raw[m][a], w_bf[m][:, a, :, :], 0, P)
+            nc.scalar.activation(dst, src, ACT.Copy)
+
+        def quantize_w(m, lo, hi):
+            nc.vector.quantize_mx(
+                out=w_words[m][:, lo:hi, :].rearrange("p a n -> p (a n)").bitcast(FP8X4),
+                scales=w_bytes[m][:, lo:hi, :].rearrange("p a n -> p (a n)"),
+                in_=w_bf[m][:, lo:hi, :, :].rearrange("p a n j -> p (a n j)"),
+            )
+
+        def layer(m):
+            parts = 2 if m == 0 else 1
+            n = S // parts
+            y[m] = keep.tile([P, S], F32, name=f"y{m}", tag=f"w_raw{m + 1}_{PASSES - 1}" if m + 1 < BLOCKS else f"y{m}")
+            for h in range(parts):
+                cols = slice(h * n, (h + 1) * n)
+                acc = psum.tile([P, n], F32, name=f"acc{m}_{h}", tag=f"acc{m}_{h}", bufs=1)
+                for a in range(PASSES):
+                    nc.tensor.matmul_mx(
+                        out=acc[:],
+                        lhsT=w_words[m][:, a, :].bitcast(FP8X4),
+                        lhsT_scale=w_bytes[m][:, a, :],
+                        rhs=got_words[a][:, cols].bitcast(FP8X4),
+                        rhs_scale=got_bytes[PACK * a :, cols],
+                        start=(a == 0),
+                        stop=(a == PASSES - 1),
+                    )
+                nc.scalar.activation(y[m][:, cols], acc[:], ACT.Identity, bias=bias[:, m : m + 1])
+
+        def term(m, d, tag):
+            terms[m, d] = keep.tile([P, V], F32, name=f"term{m}_{d}", tag=tag or f"term{m}_{d}", align_bytes=64)
+            nc.vector.tensor_tensor(terms[m, d][:], y[m][:].indirect(neigh[d][:]), gates[m][:, d, :], ALU.mult)
+
+        def sum_on_tensor(m):
+            halves = [slice(h * P, (h + 1) * P) for h in range(V // P)]
+            if m + 2 < BLOCKS:
+                across = psum.tile([P, V], F32, name=f"across{m}", tag=f"acc{m + 2}_0", bufs=1)
+                for cols in halves:
+                    for d in range(D):
+                        nc.tensor.matmul(across[:, cols], terms[m, d][:, cols], ident[:], start=(d == 0), stop=(d == D - 1), is_transpose=True)
+                nc.scalar.copy(turned[m][:], across[:])
+            else:
+                banks = [psum.tile([P, P], F32, name=f"across{m}_{h}", tag=f"acc0_{h}", bufs=1) for h in range(V // P)]
+                for d in range(D):
+                    for bank, cols in zip(banks, halves):
+                        nc.tensor.matmul(bank[:], terms[m, d][:, cols], ident[:], start=(d == 0), stop=(d == D - 1), is_transpose=True)
+                for bank, cols in zip(banks, halves):
+                    nc.scalar.copy(turned[m][:, cols], bank[:])
+            back = psum.tile([P, V], F32, name="back", tag="back")
+            for h in range(V // P):
+                nc.tensor.transpose(back[:, h * P : (h + 1) * P], turned[m][:, h * P : (h + 1) * P], ident[:])
+            nc.scalar.copy(result[m][:], back[:])
+
+        def store(m):
+            nc.sync.dma_start(out=out[m * P : (m + 1) * P, :], in_=result[m][:])
+
+        last = len(X_CHUNKS) - 1
+        for c in range(last + 1):
+            cast_x(c)
+            if c > 0:
+                quantize_x(c - 1)
+                if X_CHUNKS[c][0] != X_CHUNKS[c - 1][0]:
+                    gather_words(X_CHUNKS[c - 1][0])
+        quantize_x(last)
+        nc.vector.tensor_copy(got_bytes[:], x_bytes[:].indirect(picked[:]))
+        for a in range(PASSES):
+            cast_w(0, a)
+        quantize_w(0, 0, 2)
+        quantize_w(0, 2, 3)
+        gather_words(PASSES - 1)
+        for a in range(PASSES):
+            cast_w(1, a)
+        layer(0)
+        quantize_w(1, 0, 2)
+        quantize_w(1, 2, 3)
+        for m in range(BLOCKS):
+            ahead = m + 2
+            if ahead < BLOCKS:
+                for a in range(PASSES):
+                    cast_w(ahead, a)
+            if m + 1 < BLOCKS:
+                layer(m + 1)
+            term(m, 0, "w_bf1" if m == 0 else None)
+            term(m, 1, None)
+            term(m, 2, None)
+            if ahead < BLOCKS:
+                quantize_w(ahead, 0, 2)
+                quantize_w(ahead, 2, 3)
+            if m < PE_SUM_BLOCKS:
+                term(m, 3, f"w_bf{ahead}" if ahead < BLOCKS else None)
+            else:
+                nc.vector.tensor_tensor(turned[m][:], terms[m, 0][:], terms[m, 1][:], ALU.add)
+                term(m, 3, None)
+                nc.vector.tensor_tensor(terms[m, 0][:], turned[m][:], terms[m, 2][:], ALU.add)
+                nc.vector.tensor_tensor(result[m][:], terms[m, 0][:], terms[m, 3][:], ALU.add)
+            if m >= 1:
+                sum_on_tensor(m - 1)
+                store(m - 1)
+        store(BLOCKS - 1)

@@ -20,45 +20,40 @@ PACK = 4
 K_PASS = P * PACK
 PASSES = K // K_PASS
 BLOCKS = N // P
-RUN = 4
+PAIR = 2
+PAIRS = BLOCKS // PAIR
 
-X_CHUNKS = [
-    (0, 0, 256, 96), (0, 256, 256, 96), (0, 512, 512, 160),
-    (1, 0, 512, 160), (1, 512, 512, 160),
-    (2, 0, 256, 96), (2, 256, 256, 96), (2, 512, 256, 112), (2, 768, 128, 64), (2, 896, 128, 80),
-]
-PE_SUM_BLOCKS = 3
-
-
-def interleave_views(raw, grouped, lo, hi):
-    src = raw[:, :, lo:hi].rearrange("p j (c i) -> p c j i", i=RUN)
-    dst = grouped[:, lo:hi, :].rearrange("p (c i) j -> p c j i", i=RUN)
-    return dst, src
+X_LOADS = [(0, 0, 1024), (1, 0, 1024), (2, 0, 512), (2, 512, 256), (2, 768, 256)]
+X_STEPS = [(0, 0, 512, 256), (0, 512, 512, 256), (1, 0, 512, 256), (1, 512, 512, 256),
+           (2, 0, 512, 224), (3, 0, 256, 128), (4, 0, 256, 160)]
+W_PARTS = [[(0, 1), (1, 2), (2, 3)], [(0, 2), (2, 3)]]
 
 
 def tile_picked_sub_lin_bias_sub_e_kernel(tc, xT, w, b, gate, offs, pos1, pos2, pos3, pos4, out):
     nc = tc.nc
     with ExitStack() as ctx:
         keep = ctx.enter_context(tc.tile_pool(name="keep", bufs=1))
-        psum = ctx.enter_context(tc.psum_pool(name="psum", bufs=2))
+        psum = ctx.enter_context(tc.psum_pool(name="psum", bufs=1))
 
         picked = keep.tile([P, S // 16], U16, name="picked")
         neigh = [keep.tile([P, V // 16], U16, name=f"neigh{d}") for d in range(D)]
-        bias = keep.tile([P, BLOCKS], F32, name="bias")
-        x_raw = [keep.tile([P, PACK, n], F32, name=f"x_raw{c}") for c, (a, t0, n, nv) in enumerate(X_CHUNKS)]
-        x_bf = [keep.tile([P, n, PACK], BF16, name=f"x_bf{c}", align_bytes=64) for c, (a, t0, n, nv) in enumerate(X_CHUNKS)]
+        bias = keep.tile([P, PAIRS, PAIR], F32, name="bias")
+        x_raw = [keep.tile([P, PACK, n], F32, name=f"x_raw{c}") for c, (a, t0, n) in enumerate(X_LOADS)]
+        x_bf = [keep.tile([P, n, PACK], BF16, name=f"x_bf{c}", align_bytes=64) for c, (ld, t0, n, nv) in enumerate(X_STEPS)]
         x_words = [keep.tile([P, T], U32, name=f"x_words{a}", align_bytes=64) for a in range(PASSES)]
         x_bytes = keep.tile([P, T], U8, name="x_bytes", align_bytes=64)
         got_words = {}
         got_bytes = keep.tile([P, S], U8, name="got_bytes", align_bytes=64)
-        w_raw = [[keep.tile([P, PACK, P], F32, name=f"w_raw{m}_{a}", tag=f"w_raw{m}_{a}") for a in range(PASSES)] for m in range(BLOCKS)]
-        w_bf = [keep.tile([P, PASSES, P, PACK], BF16, name=f"w_bf{m}", tag=f"w_bf{m}", align_bytes=64) for m in range(BLOCKS)]
-        w_words = [keep.tile([P, PASSES, P], U32, name=f"w_words{m}", align_bytes=64) for m in range(BLOCKS)]
+        w_raw = [[keep.tile([P, PACK, PAIR * P], F32, name=f"w_raw{q}_{a}") for a in range(PASSES)] for q in range(PAIRS)]
+        w_bf = {}
+        for m in range(BLOCKS):
+            for lo, hi in W_PARTS[m // PAIR]:
+                w_bf[m, lo] = keep.tile([P, hi - lo, P, PACK], BF16, name=f"w_bf{m}_{lo}", tag=f"w_bf{m}_{lo}", align_bytes=64)
+        w_words = {}
         w_bytes = [keep.tile([P, PASSES, P], U8, name=f"w_bytes{m}", align_bytes=64) for m in range(BLOCKS)]
-        gates = [keep.tile([P, D, V], F32, name=f"gates{m}") for m in range(BLOCKS)]
-        y = {}
+        gates = [keep.tile([P, D, PAIR, V], F32, name=f"gates{q}") for q in range(PAIRS)]
+        y = [keep.tile([P, S], F32, name=f"y{m}") for m in range(BLOCKS)]
         terms = {}
-        bias_rows = keep.tile([P, P], F32, name="bias_rows")
         turned = [keep.tile([P, V], F32, name=f"turned{m}") for m in range(BLOCKS)]
         result = [keep.tile([P, V], F32, name=f"result{m}") for m in range(BLOCKS)]
         ident = keep.tile([P, P], F32, name="ident")
@@ -66,164 +61,193 @@ def tile_picked_sub_lin_bias_sub_e_kernel(tc, xT, w, b, gate, offs, pos1, pos2, 
         warm2 = keep.tile([P, 8], F32, name="warm2")
 
         def load_x(c):
-            a, t0, n, nv = X_CHUNKS[c]
+            a, t0, n = X_LOADS[c]
             rows = xT[a * K_PASS : (a + 1) * K_PASS, t0 : t0 + n]
             nc.sync.dma_start(out=x_raw[c][:], in_=rows.rearrange("(p j) t -> p j t", j=PACK))
 
-        def load_w(m, a):
-            rows = w[a * K_PASS : (a + 1) * K_PASS, m * P : (m + 1) * P]
-            nc.sync.dma_start(out=w_raw[m][a][:], in_=rows.rearrange("(p j) n -> p j n", j=PACK))
+        def load_w(q, a):
+            rows = w[a * K_PASS : (a + 1) * K_PASS, q * PAIR * P : (q + 1) * PAIR * P]
+            nc.sync.dma_start(out=w_raw[q][a][:], in_=rows.rearrange("(p j) n -> p j n", j=PACK))
 
-        def load_gate(m):
-            nc.sync.dma_start(out=gates[m][:], in_=gate[:, m * P : (m + 1) * P, :].rearrange("d p v -> p d v"))
+        def load_gate(q, lo, hi):
+            rows = gate[lo:hi, q * PAIR * P : (q + 1) * PAIR * P, :]
+            nc.sync.dma_start(out=gates[q][:, lo:hi, :, :], in_=rows.rearrange("d (p e) v -> p d e v", e=PAIR))
 
-        nc.vector.memset(bias_rows[:], 0.0)
-        nc.scalar.dma_start(out=bias_rows[0:BLOCKS, :], in_=b.rearrange("(m p) o -> m (p o)", p=P))
-        load_x(0)
-        load_x(1)
-        nc.sync.dma_start(picked[:], offs)
-        for c in range(2, len(X_CHUNKS)):
-            load_x(c)
-        for a in range(PASSES):
-            load_w(0, a)
         lists = (pos1, pos2, pos3, pos4)
-        nc.sync.dma_start(neigh[0][:], lists[0])
-        for a in range(PASSES):
-            load_w(1, a)
-            nc.sync.dma_start(neigh[a + 1][:], lists[a + 1])
-        for m in range(BLOCKS):
-            load_gate(m)
-            if m + 2 < BLOCKS:
-                for a in range(PASSES):
-                    load_w(m + 2, a)
+        load_x(0)
+        nc.scalar.dma_start(out=bias[:], in_=b.rearrange("(q p e) o -> p q (e o)", p=P, e=PAIR))
+        nc.sync.dma_start(picked[:], offs)
+        load_x(1)
+        load_w(0, 0)
+        for c in range(2, len(X_LOADS)):
+            load_x(c)
+        load_w(0, 1)
+        load_w(0, 2)
+        for d in range(2):
+            nc.sync.dma_start(neigh[d][:], lists[d])
+        load_gate(0, 0, 2)
+        load_w(1, 0)
+        for d in range(2, D):
+            nc.sync.dma_start(neigh[d][:], lists[d])
+        load_w(1, 1)
+        load_gate(0, 2, 3)
+        load_w(1, 2)
+        load_gate(0, 3, 4)
+        load_gate(1, 0, 2)
+        load_gate(1, 2, 4)
 
         nc.vector.memset(warm[:], 0.0)
         nc.scalar.activation(warm2[:], warm[:], ACT.Identity)
         nc.gpsimd.memset(x_bytes[:], 0)
         make_identity(nc, ident[:])
-        bias_cols = psum.tile([P, P], F32, name="bias_cols", tag="back")
-        nc.tensor.transpose(bias_cols[:], bias_rows[:], ident[:])
-        nc.vector.tensor_copy(bias[:], bias_cols[:, 0:BLOCKS])
 
         def cast_x(c):
-            a, t0, n, nv = X_CHUNKS[c]
-            dst, src = interleave_views(x_raw[c], x_bf[c], nv, n)
-            nc.scalar.activation(dst, src, ACT.Copy)
-            dst, src = interleave_views(x_raw[c], x_bf[c], 0, nv)
-            nc.vector.tensor_copy(dst, src)
+            ld, t0, n, nv = X_STEPS[c]
+            for lo, hi in ((nv, n), (0, nv)):
+                src = x_raw[ld][:, :, t0 + lo : t0 + hi].rearrange("p j (c i) -> p c j i", i=4)
+                dst = x_bf[c][:, lo:hi, :].rearrange("p (c i) j -> p c j i", i=4)
+                if lo == 0:
+                    nc.vector.tensor_copy(dst, src)
+                else:
+                    nc.scalar.activation(dst, src, ACT.Copy)
 
         def quantize_x(c):
-            a, t0, n, nv = X_CHUNKS[c]
+            ld, t0, n, nv = X_STEPS[c]
+            a, first, width = X_LOADS[ld]
+            nodes = slice(first + t0, first + t0 + n)
             nc.vector.quantize_mx(
-                out=x_words[a][:, t0 : t0 + n].bitcast(FP8X4),
-                scales=x_bytes[PACK * a :, t0 : t0 + n],
+                out=x_words[a][:, nodes].bitcast(FP8X4),
+                scales=x_bytes[PACK * a :, nodes],
                 in_=x_bf[c][:].rearrange("p t j -> p (t j)"),
             )
 
-        def gather_words(a):
-            got_words[a] = keep.tile([P, S], U32, name=f"got_words{a}", tag="w_bf0" if a == PASSES - 1 else f"got_words{a}", align_bytes=64)
-            parts = 2 if a == PASSES - 1 else 1
-            for h in range(parts):
-                n = S // parts
-                nc.vector.tensor_copy(got_words[a][:, h * n : (h + 1) * n], x_words[a][:].indirect(picked[:, h * n // 16 : (h + 1) * n // 16]))
+        def gather_words(a, after=None):
+            got_words[a] = keep.tile([P, S], U32, name=f"got_words{a}", tag=after or f"got_words{a}", align_bytes=64)
+            nc.vector.tensor_copy(got_words[a][:], x_words[a][:].indirect(picked[:]))
 
         def cast_w(m, a):
-            dst, src = interleave_views(w_raw[m][a], w_bf[m][:, a, :, :], 0, P)
+            q, e = divmod(m, PAIR)
+            lo = max(first for first, end in W_PARTS[q] if first <= a)
+            src = w_raw[q][a][:].rearrange("p j (c i e) -> p e c j i", i=2, e=PAIR)[:, e, :, :, :]
+            dst = w_bf[m, lo][:, a - lo, :, :].rearrange("p (c i) j -> p c j i", i=2)
             nc.scalar.activation(dst, src, ACT.Copy)
 
-        def quantize_w(m, lo, hi):
+        def quantize_w(m, lo, hi, after=None):
+            words = keep.tile([P, hi - lo, P], U32, name=f"w_words{m}_{lo}", tag=after or f"w_words{m}_{lo}", align_bytes=64)
+            for a in range(lo, hi):
+                w_words[m, a] = words[:, a - lo, :]
             nc.vector.quantize_mx(
-                out=w_words[m][:, lo:hi, :].rearrange("p a n -> p (a n)").bitcast(FP8X4),
+                out=words[:].rearrange("p a n -> p (a n)").bitcast(FP8X4),
                 scales=w_bytes[m][:, lo:hi, :].rearrange("p a n -> p (a n)"),
-                in_=w_bf[m][:, lo:hi, :, :].rearrange("p a n j -> p (a n j)"),
+                in_=w_bf[m, lo][:].rearrange("p a n j -> p (a n j)"),
             )
 
         def layer(m):
             parts = 2 if m == 0 else 1
             n = S // parts
-            y[m] = keep.tile([P, S], F32, name=f"y{m}", tag=f"w_raw{m + 1}_{PASSES - 1}" if m + 1 < BLOCKS else f"y{m}")
             for h in range(parts):
                 cols = slice(h * n, (h + 1) * n)
-                acc = psum.tile([P, n], F32, name=f"acc{m}_{h}", tag=f"acc{m}_{h}", bufs=1)
+                acc = psum.tile([P, n], F32, name=f"acc{m}_{h}", tag=f"acc{m}_{h}")
                 for a in range(PASSES):
                     nc.tensor.matmul_mx(
                         out=acc[:],
-                        lhsT=w_words[m][:, a, :].bitcast(FP8X4),
+                        lhsT=w_words[m, a].bitcast(FP8X4),
                         lhsT_scale=w_bytes[m][:, a, :],
                         rhs=got_words[a][:, cols].bitcast(FP8X4),
                         rhs_scale=got_bytes[PACK * a :, cols],
                         start=(a == 0),
                         stop=(a == PASSES - 1),
                     )
-                nc.scalar.activation(y[m][:, cols], acc[:], ACT.Identity, bias=bias[:, m : m + 1])
+                nc.scalar.activation(y[m][:, cols], acc[:], ACT.Identity, bias=bias[:, m // PAIR, m % PAIR : m % PAIR + 1])
 
-        def term(m, d, tag):
-            terms[m, d] = keep.tile([P, V], F32, name=f"term{m}_{d}", tag=tag or f"term{m}_{d}", align_bytes=64)
-            nc.vector.tensor_tensor(terms[m, d][:], y[m][:].indirect(neigh[d][:]), gates[m][:, d, :], ALU.mult)
+        def term(m, d, after=None):
+            terms[m, d] = keep.tile([P, V], F32, name=f"term{m}_{d}", tag=after or f"term{m}_{d}", align_bytes=64)
+            nc.vector.tensor_tensor(terms[m, d][:], y[m][:].indirect(neigh[d][:]), gates[m // PAIR][:, d, m % PAIR, :], ALU.mult)
 
-        def sum_on_tensor(m):
-            halves = [slice(h * P, (h + 1) * P) for h in range(V // P)]
-            if m + 2 < BLOCKS:
-                across = psum.tile([P, V], F32, name=f"across{m}", tag=f"acc{m + 2}_0", bufs=1)
-                for cols in halves:
-                    for d in range(D):
-                        nc.tensor.matmul(across[:, cols], terms[m, d][:, cols], ident[:], start=(d == 0), stop=(d == D - 1), is_transpose=True)
-                nc.scalar.copy(turned[m][:], across[:])
-            else:
-                banks = [psum.tile([P, P], F32, name=f"across{m}_{h}", tag=f"acc0_{h}", bufs=1) for h in range(V // P)]
-                for d in range(D):
-                    for bank, cols in zip(banks, halves):
-                        nc.tensor.matmul(bank[:], terms[m, d][:, cols], ident[:], start=(d == 0), stop=(d == D - 1), is_transpose=True)
-                for bank, cols in zip(banks, halves):
-                    nc.scalar.copy(turned[m][:, cols], bank[:])
-            back = psum.tile([P, V], F32, name="back", tag="back")
-            for h in range(V // P):
-                nc.tensor.transpose(back[:, h * P : (h + 1) * P], turned[m][:, h * P : (h + 1) * P], ident[:])
+        halves = [slice(h * P, (h + 1) * P) for h in range(V // P)]
+
+        def turn_back(m):
+            back = psum.tile([P, V], F32, name="back", bufs=2)
+            for cols in halves:
+                nc.tensor.transpose(back[:, cols], turned[m][:, cols], ident[:])
             nc.scalar.copy(result[m][:], back[:])
 
-        def store(m):
-            nc.sync.dma_start(out=out[m * P : (m + 1) * P, :], in_=result[m][:])
+        def sum_in_one_bank(m, tag):
+            across = psum.tile([P, V], F32, name=f"across{m}", tag=tag)
+            for cols in halves:
+                for d in range(D):
+                    nc.tensor.matmul(across[:, cols], terms[m, d][:, cols], ident[:], start=(d == 0), stop=(d == D - 1), is_transpose=True)
+            nc.scalar.copy(turned[m][:], across[:])
+            turn_back(m)
 
-        last = len(X_CHUNKS) - 1
-        for c in range(last + 1):
+        def sum_in_two_banks(m):
+            banks = [psum.tile([P, P], F32, name=f"across{m}_{h}", tag=f"acc0_{h}") for h in range(V // P)]
+            for d in range(D):
+                for bank, cols in zip(banks, halves):
+                    nc.tensor.matmul(bank[:], terms[m, d][:, cols], ident[:], start=(d == 0), stop=(d == D - 1), is_transpose=True)
+            for bank, cols in zip(banks, halves):
+                nc.scalar.copy(turned[m][:, cols], bank[:])
+            turn_back(m)
+
+        def store(m):
+            q, e = divmod(m, PAIR)
+            rows = out[q * PAIR * P : (q + 1) * PAIR * P, :].rearrange("(p e) v -> p e v", e=PAIR)
+            nc.sync.dma_start(out=rows[:, e, :], in_=result[m][:])
+
+        for c in range(len(X_STEPS)):
             cast_x(c)
             if c > 0:
                 quantize_x(c - 1)
-                if X_CHUNKS[c][0] != X_CHUNKS[c - 1][0]:
-                    gather_words(X_CHUNKS[c - 1][0])
-        quantize_x(last)
+                before, now = X_LOADS[X_STEPS[c - 1][0]][0], X_LOADS[X_STEPS[c][0]][0]
+                if before != now:
+                    gather_words(before)
+                    if now == PASSES - 1:
+                        for m in range(PAIR):
+                            cast_w(m, 0)
+                        for m in range(PAIR):
+                            quantize_w(m, 0, 1)
+        quantize_x(len(X_STEPS) - 1)
         nc.vector.tensor_copy(got_bytes[:], x_bytes[:].indirect(picked[:]))
-        for a in range(PASSES):
-            cast_w(0, a)
-        quantize_w(0, 0, 2)
+        for a in range(1, PASSES):
+            for m in range(PAIR):
+                cast_w(m, a)
+        quantize_w(0, 1, 2)
+        gather_words(PASSES - 1, "w_bf0_1")
         quantize_w(0, 2, 3)
-        gather_words(PASSES - 1)
-        for a in range(PASSES):
-            cast_w(1, a)
-        layer(0)
-        quantize_w(1, 0, 2)
+        quantize_w(1, 1, 2, "w_bf0_2")
         quantize_w(1, 2, 3)
-        for m in range(BLOCKS):
-            ahead = m + 2
-            if ahead < BLOCKS:
-                for a in range(PASSES):
-                    cast_w(ahead, a)
-            if m + 1 < BLOCKS:
-                layer(m + 1)
-            term(m, 0, "w_bf1" if m == 0 else None)
-            term(m, 1, None)
-            term(m, 2, None)
-            if ahead < BLOCKS:
-                quantize_w(ahead, 0, 2)
-                quantize_w(ahead, 2, 3)
-            if m < PE_SUM_BLOCKS:
-                term(m, 3, f"w_bf{ahead}" if ahead < BLOCKS else None)
-            else:
-                nc.vector.tensor_tensor(turned[m][:], terms[m, 0][:], terms[m, 1][:], ALU.add)
-                term(m, 3, None)
-                nc.vector.tensor_tensor(terms[m, 0][:], turned[m][:], terms[m, 2][:], ALU.add)
-                nc.vector.tensor_tensor(result[m][:], terms[m, 0][:], terms[m, 3][:], ALU.add)
-            if m >= 1:
-                sum_on_tensor(m - 1)
-                store(m - 1)
-        store(BLOCKS - 1)
+        layer(0)
+        layer(1)
+        for a in range(PASSES):
+            for m in range(PAIR, BLOCKS):
+                cast_w(m, a)
+        term(0, 0, "w_bf1_2")
+        term(0, 1)
+        term(1, 0)
+        term(1, 1)
+        term(0, 2)
+        quantize_w(2, 0, 2)
+        term(1, 2, "w_bf2_0")
+        quantize_w(2, 2, 3)
+        layer(2)
+        quantize_w(3, 0, 2, "w_bf2_2")
+        term(0, 3, "w_bf3_0")
+        quantize_w(3, 2, 3)
+        layer(3)
+        term(1, 3, "w_bf3_2")
+        for d in range(D):
+            term(2, d)
+        m = BLOCKS - 1
+        for d in range(D - 1):
+            term(m, d)
+        nc.vector.tensor_tensor(turned[m][:], terms[m, 0][:], terms[m, 1][:], ALU.add)
+        term(m, D - 1)
+        nc.vector.tensor_tensor(terms[m, 0][:], turned[m][:], terms[m, 2][:], ALU.add)
+        nc.vector.tensor_tensor(result[m][:], terms[m, 0][:], terms[m, 3][:], ALU.add)
+        sum_in_one_bank(0, "acc2_0")
+        store(0)
+        sum_in_one_bank(1, "acc1_0")
+        store(1)
+        sum_in_two_banks(2)
+        store(2)
+        store(3)

@@ -24,8 +24,9 @@ PAIR = 2
 PAIRS = BLOCKS // PAIR
 
 X_LOADS = [(0, 0, 1024), (1, 0, 1024), (2, 0, 512), (2, 512, 256), (2, 768, 256)]
-X_STEPS = [(0, 0, 512, 256), (0, 512, 512, 256), (1, 0, 512, 256), (1, 512, 512, 256),
-           (2, 0, 512, 224), (3, 0, 256, 128), (4, 0, 256, 160)]
+X_STEPS = [(0, 0, 512, 256), (0, 512, 512, 256), (1, 0, 512, 320), (1, 512, 512, 320),
+           (2, 0, 512, 128), (3, 0, 256, 64), (4, 0, 256, 160)]
+SUM_BANKS = [("acc0_0", "acc0_1"), ("acc1_0", "spare"), ("acc0_0", "acc0_1")]
 W_PARTS = [[(0, 1), (1, 2), (2, 3)], [(0, 2), (2, 3)]]
 
 
@@ -172,22 +173,19 @@ def tile_picked_sub_lin_bias_sub_e_kernel(tc, xT, w, b, gate, offs, pos1, pos2, 
                 nc.tensor.transpose(back[:, cols], turned[m][:, cols], ident[:])
             nc.scalar.copy(result[m][:], back[:])
 
-        def sum_in_one_bank(m, tag):
-            across = psum.tile([P, V], F32, name=f"across{m}", tag=tag)
-            for cols in halves:
-                for d in range(D):
-                    nc.tensor.matmul(across[:, cols], terms[m, d][:, cols], ident[:], start=(d == 0), stop=(d == D - 1), is_transpose=True)
-            nc.scalar.copy(turned[m][:], across[:])
-            turn_back(m)
+        across = {}
 
-        def sum_in_two_banks(m):
-            banks = [psum.tile([P, P], F32, name=f"across{m}_{h}", tag=f"acc0_{h}") for h in range(V // P)]
-            for d in range(D):
-                for bank, cols in zip(banks, halves):
-                    nc.tensor.matmul(bank[:], terms[m, d][:, cols], ident[:], start=(d == 0), stop=(d == D - 1), is_transpose=True)
-            for bank, cols in zip(banks, halves):
-                nc.scalar.copy(turned[m][:, cols], bank[:])
+        def add_turned(m, d):
+            for h, cols in enumerate(halves):
+                if d == 0:
+                    across[m, h] = psum.tile([P, P], F32, name=f"across{m}_{h}", tag=SUM_BANKS[m][h])
+                nc.tensor.matmul(across[m, h][:], terms[m, d][:, cols], ident[:], start=(d == 0), stop=(d == D - 1), is_transpose=True)
+
+        def finish_sum(m):
+            for h, cols in enumerate(halves):
+                nc.scalar.copy(turned[m][:, cols], across[m, h][:])
             turn_back(m)
+            store(m)
 
         def store(m):
             q, e = divmod(m, PAIR)
@@ -240,14 +238,20 @@ def tile_picked_sub_lin_bias_sub_e_kernel(tc, xT, w, b, gate, offs, pos1, pos2, 
         m = BLOCKS - 1
         for d in range(D - 1):
             term(m, d)
+        last = keep.tile([P, V], F32, name="last")
         nc.vector.tensor_tensor(turned[m][:], terms[m, 0][:], terms[m, 1][:], ALU.add)
-        term(m, D - 1)
-        nc.vector.tensor_tensor(terms[m, 0][:], turned[m][:], terms[m, 2][:], ALU.add)
-        nc.vector.tensor_tensor(result[m][:], terms[m, 0][:], terms[m, 3][:], ALU.add)
-        sum_in_one_bank(0, "acc2_0")
-        store(0)
-        sum_in_one_bank(1, "acc1_0")
-        store(1)
-        sum_in_two_banks(2)
-        store(2)
+        for h, cols in enumerate(halves):
+            nc.vector.tensor_tensor(last[:, cols], y[m][:].indirect(neigh[D - 1][:, h * P // 16 : (h + 1) * P // 16]), gates[m // PAIR][:, D - 1, m % PAIR, cols], ALU.mult)
+            if h == 0:
+                nc.vector.tensor_tensor(terms[m, 0][:], turned[m][:], terms[m, 2][:], ALU.add)
+        for cols in halves:
+            nc.vector.tensor_tensor(result[m][:, cols], terms[m, 0][:, cols], last[:, cols], ALU.add)
+        for d in range(D):
+            for m in range(PAIR):
+                add_turned(m, d)
+        finish_sum(0)
+        finish_sum(1)
+        for d in range(D):
+            add_turned(2, d)
+        finish_sum(2)
         store(3)

@@ -38,7 +38,8 @@ def tile_picked_sub_lin_bias_sub_e_kernel(tc, xT, w, b, gate, offs, pos1, pos2, 
 
         picked = keep.tile([P, S // 16], U16, name="picked")
         neigh = [keep.tile([P, V // 16], U16, name=f"neigh{d}") for d in range(D)]
-        bias = keep.tile([P, PAIRS, PAIR], F32, name="bias")
+        bias = keep.tile([P, BLOCKS], F32, name="bias")
+        bias_rows = keep.tile([P, P], F32, name="bias_rows")
         x_raw = [keep.tile([P, PACK, n], F32, name=f"x_raw{c}") for c, (a, t0, n) in enumerate(X_LOADS)]
         x_bf = [keep.tile([P, n, PACK], BF16, name=f"x_bf{c}", align_bytes=64) for c, (ld, t0, n, nv) in enumerate(X_STEPS)]
         x_words = [keep.tile([P, T], U32, name=f"x_words{a}", align_bytes=64) for a in range(PASSES)]
@@ -70,13 +71,18 @@ def tile_picked_sub_lin_bias_sub_e_kernel(tc, xT, w, b, gate, offs, pos1, pos2, 
             rows = w[a * K_PASS : (a + 1) * K_PASS, q * PAIR * P : (q + 1) * PAIR * P]
             nc.sync.dma_start(out=w_raw[q][a][:], in_=rows.rearrange("(p j) n -> p j n", j=PACK))
 
-        def load_gate(q, lo, hi):
-            rows = gate[lo:hi, q * PAIR * P : (q + 1) * PAIR * P, :]
-            nc.sync.dma_start(out=gates[q][:, lo:hi, :, :], in_=rows.rearrange("d (p e) v -> p d e v", e=PAIR))
+        def load_gate_turns(m, lo, hi):
+            rows = gate[lo:hi, m * P : (m + 1) * P, :]
+            nc.sync.dma_start(out=gates[m // PAIR][:, lo:hi, m % PAIR, :], in_=rows.rearrange("d p v -> p d v"))
+
+        def load_gate_pair(q, d):
+            rows = gate[d, q * PAIR * P : (q + 1) * PAIR * P, :]
+            nc.sync.dma_start(out=gates[q][:, d, :, :], in_=rows.rearrange("(e p) v -> p e v", p=P))
 
         lists = (pos1, pos2, pos3, pos4)
         load_x(0)
-        nc.scalar.dma_start(out=bias[:], in_=b.rearrange("(q p e) o -> p q (e o)", p=P, e=PAIR))
+        nc.vector.memset(bias_rows[:], 0.0)
+        nc.scalar.dma_start(out=bias_rows[0:BLOCKS, :], in_=b.rearrange("(m p) o -> m (p o)", p=P))
         nc.sync.dma_start(picked[:], offs)
         load_x(1)
         load_w(0, 0)
@@ -86,21 +92,25 @@ def tile_picked_sub_lin_bias_sub_e_kernel(tc, xT, w, b, gate, offs, pos1, pos2, 
         load_w(0, 2)
         for d in range(2):
             nc.sync.dma_start(neigh[d][:], lists[d])
-        load_gate(0, 0, 2)
+        load_gate_turns(0, 0, 2)
+        load_gate_turns(1, 0, 2)
         load_w(1, 0)
         for d in range(2, D):
             nc.sync.dma_start(neigh[d][:], lists[d])
         load_w(1, 1)
-        load_gate(0, 2, 3)
+        load_gate_pair(0, 2)
         load_w(1, 2)
-        load_gate(0, 3, 4)
-        load_gate(1, 0, 2)
-        load_gate(1, 2, 4)
+        load_gate_pair(0, 3)
+        load_gate_turns(2, 0, D)
+        load_gate_turns(3, 0, D)
 
         nc.vector.memset(warm[:], 0.0)
         nc.scalar.activation(warm2[:], warm[:], ACT.Identity)
         nc.gpsimd.memset(x_bytes[:], 0)
         make_identity(nc, ident[:])
+        bias_cols = psum.tile([P, P], F32, name="bias_cols", tag="spare")
+        nc.tensor.transpose(bias_cols[:], bias_rows[:], ident[:])
+        nc.vector.tensor_copy(bias[:], bias_cols[:, 0:BLOCKS])
 
         def cast_x(c):
             ld, t0, n, nv = X_STEPS[c]
@@ -129,8 +139,8 @@ def tile_picked_sub_lin_bias_sub_e_kernel(tc, xT, w, b, gate, offs, pos1, pos2, 
         def cast_w(m, a):
             q, e = divmod(m, PAIR)
             lo = max(first for first, end in W_PARTS[q] if first <= a)
-            src = w_raw[q][a][:].rearrange("p j (c i e) -> p e c j i", i=2, e=PAIR)[:, e, :, :, :]
-            dst = w_bf[m, lo][:, a - lo, :, :].rearrange("p (c i) j -> p c j i", i=2)
+            src = w_raw[q][a][:, :, e * P : (e + 1) * P].rearrange("p j (c i) -> p c j i", i=4)
+            dst = w_bf[m, lo][:, a - lo, :, :].rearrange("p (c i) j -> p c j i", i=4)
             nc.scalar.activation(dst, src, ACT.Copy)
 
         def quantize_w(m, lo, hi, after=None):
@@ -159,7 +169,7 @@ def tile_picked_sub_lin_bias_sub_e_kernel(tc, xT, w, b, gate, offs, pos1, pos2, 
                         start=(a == 0),
                         stop=(a == PASSES - 1),
                     )
-                nc.scalar.activation(y[m][:, cols], acc[:], ACT.Identity, bias=bias[:, m // PAIR, m % PAIR : m % PAIR + 1])
+                nc.scalar.activation(y[m][:, cols], acc[:], ACT.Identity, bias=bias[:, m : m + 1])
 
         def term(m, d, after=None):
             terms[m, d] = keep.tile([P, V], F32, name=f"term{m}_{d}", tag=after or f"term{m}_{d}", align_bytes=64)
@@ -188,9 +198,7 @@ def tile_picked_sub_lin_bias_sub_e_kernel(tc, xT, w, b, gate, offs, pos1, pos2, 
             store(m)
 
         def store(m):
-            q, e = divmod(m, PAIR)
-            rows = out[q * PAIR * P : (q + 1) * PAIR * P, :].rearrange("(p e) v -> p e v", e=PAIR)
-            nc.sync.dma_start(out=rows[:, e, :], in_=result[m][:])
+            nc.sync.dma_start(out=out[m * P : (m + 1) * P, :], in_=result[m][:])
 
         for c in range(len(X_STEPS)):
             cast_x(c)
@@ -238,14 +246,10 @@ def tile_picked_sub_lin_bias_sub_e_kernel(tc, xT, w, b, gate, offs, pos1, pos2, 
         m = BLOCKS - 1
         for d in range(D - 1):
             term(m, d)
-        last = keep.tile([P, V], F32, name="last")
         nc.vector.tensor_tensor(turned[m][:], terms[m, 0][:], terms[m, 1][:], ALU.add)
-        for h, cols in enumerate(halves):
-            nc.vector.tensor_tensor(last[:, cols], y[m][:].indirect(neigh[D - 1][:, h * P // 16 : (h + 1) * P // 16]), gates[m // PAIR][:, D - 1, m % PAIR, cols], ALU.mult)
-            if h == 0:
-                nc.vector.tensor_tensor(terms[m, 0][:], turned[m][:], terms[m, 2][:], ALU.add)
-        for cols in halves:
-            nc.vector.tensor_tensor(result[m][:, cols], terms[m, 0][:, cols], last[:, cols], ALU.add)
+        term(m, D - 1)
+        nc.vector.tensor_tensor(terms[m, 0][:], turned[m][:], terms[m, 2][:], ALU.add)
+        nc.vector.tensor_tensor(result[m][:], terms[m, 0][:], terms[m, 3][:], ALU.add)
         for d in range(D):
             for m in range(PAIR):
                 add_turned(m, d)

@@ -5,6 +5,7 @@ from concourse.masks import make_identity
 
 K, T, D, S, V, N = 1536, 1024, 4, 512, 256, 512
 FLOPS = 2 * K * N * S
+BYTES = 4 * (K * T + K * N + N + D * V + N * V) + 2 * 128 * (S + D * V) // 16
 
 F32 = mybir.dt.float32
 BF16 = mybir.dt.bfloat16
@@ -20,14 +21,12 @@ PACK = 4
 K_PASS = P * PACK
 PASSES = K // K_PASS
 BLOCKS = N // P
-PAIR = 2
-PAIRS = BLOCKS // PAIR
+HALVES = V // P
 
-X_LOADS = [(0, 0, 1024), (1, 0, 1024), (2, 0, 512), (2, 512, 256), (2, 768, 256)]
-X_STEPS = [(0, 0, 512, 256), (0, 512, 512, 256), (1, 0, 512, 320), (1, 512, 512, 320),
-           (2, 0, 512, 128), (3, 0, 256, 64), (4, 0, 256, 160)]
-SUM_BANKS = [("acc0_0", "acc0_1"), ("acc1_0", "spare"), ("acc0_0", "acc0_1")]
-W_PARTS = [[(0, 1), (1, 2), (2, 3)], [(0, 2), (2, 3)]]
+X_PIECES = [(0, 0, 512, 192), (0, 512, 512, 192), (1, 0, 512, 128), (1, 512, 512, 192),
+            (2, 0, 512, 64), (2, 512, 256, 64), (2, 768, 256, 160)]
+W_PARTS = [(0, 2), (2, 3)]
+EARLY_TERMS = [2, 1, 1]
 
 
 def tile_picked_sub_lin_bias_sub_e_kernel(tc, xT, w, b, gate, offs, pos1, pos2, pos3, pos4, out):
@@ -38,84 +37,76 @@ def tile_picked_sub_lin_bias_sub_e_kernel(tc, xT, w, b, gate, offs, pos1, pos2, 
 
         picked = keep.tile([P, S // 16], U16, name="picked")
         neigh = [keep.tile([P, V // 16], U16, name=f"neigh{d}") for d in range(D)]
-        bias = keep.tile([P, BLOCKS], F32, name="bias")
-        bias_rows = keep.tile([P, P], F32, name="bias_rows")
-        x_raw = [keep.tile([P, PACK, n], F32, name=f"x_raw{c}") for c, (a, t0, n) in enumerate(X_LOADS)]
-        x_bf = [keep.tile([P, n, PACK], BF16, name=f"x_bf{c}", align_bytes=64) for c, (ld, t0, n, nv) in enumerate(X_STEPS)]
+        small_rows = keep.tile([P, V], F32, name="small_rows")
+        small_cols = keep.tile([P, HALVES, 8], F32, name="small_cols")
+        gates = keep.tile([P, D, V], F32, name="gates")
+        x_raw = [keep.tile([P, PACK, n], F32, name=f"x_raw{c}") for c, (a, t0, n, nv) in enumerate(X_PIECES)]
+        x_bf = [keep.tile([P, n, PACK], BF16, name=f"x_bf{c}", align_bytes=64) for c, (a, t0, n, nv) in enumerate(X_PIECES)]
         x_words = [keep.tile([P, T], U32, name=f"x_words{a}", align_bytes=64) for a in range(PASSES)]
         x_bytes = keep.tile([P, T], U8, name="x_bytes", align_bytes=64)
         got_words = {}
         got_bytes = keep.tile([P, S], U8, name="got_bytes", align_bytes=64)
-        w_raw = [[keep.tile([P, PACK, PAIR * P], F32, name=f"w_raw{q}_{a}") for a in range(PASSES)] for q in range(PAIRS)]
-        w_bf = {}
+        w_raw, w_bf, w_words, w_bytes = {}, {}, {}, {}
         for m in range(BLOCKS):
-            for lo, hi in W_PARTS[m // PAIR]:
+            for a in range(PASSES):
+                w_raw[m, a] = keep.tile([P, PACK, P], F32, name=f"w_raw{m}_{a}", tag=f"w_raw{m}_{a}", align_bytes=64)
+            for lo, hi in W_PARTS:
                 w_bf[m, lo] = keep.tile([P, hi - lo, P, PACK], BF16, name=f"w_bf{m}_{lo}", tag=f"w_bf{m}_{lo}", align_bytes=64)
-        w_words = {}
-        w_bytes = [keep.tile([P, PASSES, P], U8, name=f"w_bytes{m}", align_bytes=64) for m in range(BLOCKS)]
-        gates = [keep.tile([P, D, PAIR, V], F32, name=f"gates{q}") for q in range(PAIRS)]
+                w_words[m, lo] = keep.tile([P, hi - lo, P], U32, name=f"w_words{m}_{lo}", align_bytes=64)
+                w_bytes[m, lo] = keep.tile([P, hi - lo, P], U8, name=f"w_bytes{m}_{lo}", align_bytes=64)
         y = [keep.tile([P, S], F32, name=f"y{m}") for m in range(BLOCKS)]
         terms = {}
-        turned = [keep.tile([P, V], F32, name=f"turned{m}") for m in range(BLOCKS)]
         result = [keep.tile([P, V], F32, name=f"result{m}") for m in range(BLOCKS)]
+        partial = [keep.tile([P, V], F32, name=f"partial{i}") for i in range(2)]
         ident = keep.tile([P, P], F32, name="ident")
-        warm = keep.tile([P, 8], F32, name="warm")
-        warm2 = keep.tile([P, 8], F32, name="warm2")
 
         def load_x(c):
-            a, t0, n = X_LOADS[c]
+            a, t0, n, nv = X_PIECES[c]
             rows = xT[a * K_PASS : (a + 1) * K_PASS, t0 : t0 + n]
             nc.sync.dma_start(out=x_raw[c][:], in_=rows.rearrange("(p j) t -> p j t", j=PACK))
 
-        def load_w(q, a):
-            rows = w[a * K_PASS : (a + 1) * K_PASS, q * PAIR * P : (q + 1) * PAIR * P]
-            nc.sync.dma_start(out=w_raw[q][a][:], in_=rows.rearrange("(p j) n -> p j n", j=PACK))
-
-        def load_gate_turns(m, lo, hi):
-            rows = gate[lo:hi, m * P : (m + 1) * P, :]
-            nc.sync.dma_start(out=gates[m // PAIR][:, lo:hi, m % PAIR, :], in_=rows.rearrange("d p v -> p d v"))
-
-        def load_gate_pair(q, d):
-            rows = gate[d, q * PAIR * P : (q + 1) * PAIR * P, :]
-            nc.sync.dma_start(out=gates[q][:, d, :, :], in_=rows.rearrange("(e p) v -> p e v", p=P))
+        def load_w(m, a):
+            rows = w[a * K_PASS : (a + 1) * K_PASS, m * P : (m + 1) * P]
+            nc.sync.dma_start(out=w_raw[m, a][:], in_=rows.rearrange("(p j) n -> p j n", j=PACK))
 
         lists = (pos1, pos2, pos3, pos4)
+        nc.gpsimd.memset(small_rows[:], 0.0)
         load_x(0)
-        nc.vector.memset(bias_rows[:], 0.0)
-        nc.scalar.dma_start(out=bias_rows[0:BLOCKS, :], in_=b.rearrange("(m p) o -> m (p o)", p=P))
+        nc.sync.dma_start(out=small_rows[0:D, :], in_=gate[:, 0, :])
+        nc.sync.dma_start(out=small_rows[D : D + 2, :], in_=b.rearrange("(e q) o -> e (q o)", e=2))
         nc.sync.dma_start(picked[:], offs)
-        load_x(1)
-        load_w(0, 0)
-        for c in range(2, len(X_LOADS)):
+        for c in range(1, len(X_PIECES)):
             load_x(c)
-        load_w(0, 1)
-        load_w(0, 2)
-        for d in range(2):
-            nc.sync.dma_start(neigh[d][:], lists[d])
-        load_gate_turns(0, 0, 2)
-        load_gate_turns(1, 0, 2)
-        load_w(1, 0)
-        for d in range(2, D):
-            nc.sync.dma_start(neigh[d][:], lists[d])
-        load_w(1, 1)
-        load_gate_pair(0, 2)
-        load_w(1, 2)
-        load_gate_pair(0, 3)
-        load_gate_turns(2, 0, D)
-        load_gate_turns(3, 0, D)
+        for m in range(BLOCKS):
+            for a in range(PASSES):
+                load_w(m, a)
+            if m == 0:
+                for d in range(D):
+                    nc.sync.dma_start(neigh[d][:], lists[d])
 
-        nc.vector.memset(warm[:], 0.0)
-        nc.scalar.activation(warm2[:], warm[:], ACT.Identity)
         nc.gpsimd.memset(x_bytes[:], 0)
         make_identity(nc, ident[:])
-        bias_cols = psum.tile([P, P], F32, name="bias_cols", tag="spare")
-        nc.tensor.transpose(bias_cols[:], bias_rows[:], ident[:])
-        nc.vector.tensor_copy(bias[:], bias_cols[:, 0:BLOCKS])
+        halves = [slice(h * P, (h + 1) * P) for h in range(HALVES)]
+        cols_ps = psum.tile([P, HALVES, P], F32, name="cols_ps", tag="across0")
+        for h in range(HALVES):
+            nc.tensor.transpose(cols_ps[:, h, :], small_rows[:, halves[h]], ident[:])
+        nc.scalar.copy(small_cols[:], cols_ps[:, :, 0:8])
+        for q in range(D // 2):
+            spread = psum.tile([P, 2, V], F32, name=f"spread{q}", tag=f"back{q}")
+            for e in range(2):
+                for h in range(HALVES):
+                    column = small_cols[:, h, 2 * q + e : 2 * q + e + 1]
+                    nc.tensor.transpose(spread[:, e, halves[h]], column.to_broadcast([P, P]), ident[:])
+            nc.vector.tensor_copy(gates[:, 2 * q : 2 * q + 2, :], spread[:])
+
+        def bias(m):
+            e, h = divmod(m, HALVES)
+            return small_cols[:, h, D + e : D + e + 1]
 
         def cast_x(c):
-            ld, t0, n, nv = X_STEPS[c]
+            a, t0, n, nv = X_PIECES[c]
             for lo, hi in ((nv, n), (0, nv)):
-                src = x_raw[ld][:, :, t0 + lo : t0 + hi].rearrange("p j (c i) -> p c j i", i=4)
+                src = x_raw[c][:, :, lo:hi].rearrange("p j (c i) -> p c j i", i=4)
                 dst = x_bf[c][:, lo:hi, :].rearrange("p (c i) j -> p c j i", i=4)
                 if lo == 0:
                     nc.vector.tensor_copy(dst, src)
@@ -123,139 +114,115 @@ def tile_picked_sub_lin_bias_sub_e_kernel(tc, xT, w, b, gate, offs, pos1, pos2, 
                     nc.scalar.activation(dst, src, ACT.Copy)
 
         def quantize_x(c):
-            ld, t0, n, nv = X_STEPS[c]
-            a, first, width = X_LOADS[ld]
-            nodes = slice(first + t0, first + t0 + n)
+            a, t0, n, nv = X_PIECES[c]
             nc.vector.quantize_mx(
-                out=x_words[a][:, nodes].bitcast(FP8X4),
-                scales=x_bytes[PACK * a :, nodes],
+                out=x_words[a][:, t0 : t0 + n].bitcast(FP8X4),
+                scales=x_bytes[PACK * a :, t0 : t0 + n],
                 in_=x_bf[c][:].rearrange("p t j -> p (t j)"),
             )
 
-        def gather_words(a, after=None):
-            got_words[a] = keep.tile([P, S], U32, name=f"got_words{a}", tag=after or f"got_words{a}", align_bytes=64)
-            nc.vector.tensor_copy(got_words[a][:], x_words[a][:].indirect(picked[:]))
+        def gather_words(a):
+            got = keep.tile([P, S], U32, name=f"got_words{a}", align_bytes=64)
+            nc.vector.tensor_copy(got[:], x_words[a][:].indirect(picked[:]))
+            for h in range(2):
+                got_words[a, h] = got[:, h * S // 2 : (h + 1) * S // 2]
+
+        def gather_half(a, h, after):
+            got = keep.tile([P, S // 2], U32, name=f"got_words{a}_{h}", tag=after, align_bytes=64)
+            nc.vector.tensor_copy(got[:], x_words[a][:].indirect(picked[:, h * S // 32 : (h + 1) * S // 32]))
+            got_words[a, h] = got[:]
 
         def cast_w(m, a):
-            q, e = divmod(m, PAIR)
-            lo = max(first for first, end in W_PARTS[q] if first <= a)
-            src = w_raw[q][a][:, :, e * P : (e + 1) * P].rearrange("p j (c i) -> p c j i", i=4)
+            src = w_raw[m, a][:].rearrange("p j (c i) -> p c j i", i=4)
+            lo = max(first for first, end in W_PARTS if first <= a)
             dst = w_bf[m, lo][:, a - lo, :, :].rearrange("p (c i) j -> p c j i", i=4)
             nc.scalar.activation(dst, src, ACT.Copy)
 
-        def quantize_w(m, lo, hi, after=None):
-            words = keep.tile([P, hi - lo, P], U32, name=f"w_words{m}_{lo}", tag=after or f"w_words{m}_{lo}", align_bytes=64)
-            for a in range(lo, hi):
-                w_words[m, a] = words[:, a - lo, :]
+        def quantize_w(m, lo):
             nc.vector.quantize_mx(
-                out=words[:].rearrange("p a n -> p (a n)").bitcast(FP8X4),
-                scales=w_bytes[m][:, lo:hi, :].rearrange("p a n -> p (a n)"),
+                out=w_words[m, lo][:].rearrange("p a n -> p (a n)").bitcast(FP8X4),
+                scales=w_bytes[m, lo][:].rearrange("p a n -> p (a n)"),
                 in_=w_bf[m, lo][:].rearrange("p a n j -> p (a n j)"),
             )
 
         def layer(m):
-            parts = 2 if m == 0 else 1
-            n = S // parts
-            for h in range(parts):
-                cols = slice(h * n, (h + 1) * n)
-                acc = psum.tile([P, n], F32, name=f"acc{m}_{h}", tag=f"acc{m}_{h}")
-                for a in range(PASSES):
+            n = S // 2
+            accs = [psum.tile([P, n], F32, name=f"acc{m}_{h}", tag=f"acc{m % 2}_{h}") for h in range(2)]
+            for a in range(PASSES):
+                lo = max(first for first, end in W_PARTS if first <= a)
+                for h in range(2):
+                    cols = slice(h * n, (h + 1) * n)
                     nc.tensor.matmul_mx(
-                        out=acc[:],
-                        lhsT=w_words[m, a].bitcast(FP8X4),
-                        lhsT_scale=w_bytes[m][:, a, :],
-                        rhs=got_words[a][:, cols].bitcast(FP8X4),
+                        out=accs[h][:],
+                        lhsT=w_words[m, lo][:, a - lo, :].bitcast(FP8X4),
+                        lhsT_scale=w_bytes[m, lo][:, a - lo, :],
+                        rhs=got_words[a, h].bitcast(FP8X4),
                         rhs_scale=got_bytes[PACK * a :, cols],
                         start=(a == 0),
                         stop=(a == PASSES - 1),
                     )
-                nc.scalar.activation(y[m][:, cols], acc[:], ACT.Identity, bias=bias[:, m : m + 1])
+            for h in range(2):
+                nc.scalar.activation(y[m][:, h * n : (h + 1) * n], accs[h][:], ACT.Identity, bias=bias(m))
 
-        def term(m, d, after=None):
-            terms[m, d] = keep.tile([P, V], F32, name=f"term{m}_{d}", tag=after or f"term{m}_{d}", align_bytes=64)
-            nc.vector.tensor_tensor(terms[m, d][:], y[m][:].indirect(neigh[d][:]), gates[m // PAIR][:, d, m % PAIR, :], ALU.mult)
+        def term(m, d, dst):
+            terms[m, d] = dst
+            nc.vector.tensor_tensor(dst, y[m][:].indirect(neigh[d][:]), gates[:, d, :], ALU.mult)
 
-        halves = [slice(h * P, (h + 1) * P) for h in range(V // P)]
-
-        def turn_back(m):
-            back = psum.tile([P, V], F32, name="back", bufs=2)
+        def sum_terms(m):
+            across = psum.tile([P, V], F32, name=f"across{m}", tag="across0")
             for cols in halves:
-                nc.tensor.transpose(back[:, cols], turned[m][:, cols], ident[:])
+                for d in range(D):
+                    nc.tensor.matmul(across[:, cols], terms[m, d][:, cols], ident[:], start=(d == 0), stop=(d == D - 1), is_transpose=True)
+            hold = f"w_bf{m + 2}_{PASSES - 1}" if m + 2 < BLOCKS else f"turned{m}"
+            turned = keep.tile([P, V], F32, name=f"turned{m}", tag=hold, align_bytes=64)
+            nc.scalar.copy(turned[:], across[:])
+            back = psum.tile([P, V], F32, name=f"back{m}", tag=f"back{m % 2}")
+            for cols in halves:
+                nc.tensor.transpose(back[:, cols], turned[:, cols], ident[:])
             nc.scalar.copy(result[m][:], back[:])
-
-        across = {}
-
-        def add_turned(m, d):
-            for h, cols in enumerate(halves):
-                if d == 0:
-                    across[m, h] = psum.tile([P, P], F32, name=f"across{m}_{h}", tag=SUM_BANKS[m][h])
-                nc.tensor.matmul(across[m, h][:], terms[m, d][:, cols], ident[:], start=(d == 0), stop=(d == D - 1), is_transpose=True)
-
-        def finish_sum(m):
-            for h, cols in enumerate(halves):
-                nc.scalar.copy(turned[m][:, cols], across[m, h][:])
-            turn_back(m)
             store(m)
 
         def store(m):
             nc.sync.dma_start(out=out[m * P : (m + 1) * P, :], in_=result[m][:])
 
-        for c in range(len(X_STEPS)):
+        for c in range(len(X_PIECES)):
             cast_x(c)
             if c > 0:
                 quantize_x(c - 1)
-                before, now = X_LOADS[X_STEPS[c - 1][0]][0], X_LOADS[X_STEPS[c][0]][0]
+                before, now = X_PIECES[c - 1][0], X_PIECES[c][0]
                 if before != now:
                     gather_words(before)
-                    if now == PASSES - 1:
-                        for m in range(PAIR):
-                            cast_w(m, 0)
-                        for m in range(PAIR):
-                            quantize_w(m, 0, 1)
-        quantize_x(len(X_STEPS) - 1)
+        quantize_x(len(X_PIECES) - 1)
         nc.vector.tensor_copy(got_bytes[:], x_bytes[:].indirect(picked[:]))
-        for a in range(1, PASSES):
-            for m in range(PAIR):
-                cast_w(m, a)
-        quantize_w(0, 1, 2)
-        gather_words(PASSES - 1, "w_bf0_1")
-        quantize_w(0, 2, 3)
-        quantize_w(1, 1, 2, "w_bf0_2")
-        quantize_w(1, 2, 3)
-        layer(0)
-        layer(1)
         for a in range(PASSES):
-            for m in range(PAIR, BLOCKS):
-                cast_w(m, a)
-        term(0, 0, "w_bf1_2")
-        term(0, 1)
-        term(1, 0)
-        term(1, 1)
-        term(0, 2)
-        quantize_w(2, 0, 2)
-        term(1, 2, "w_bf2_0")
-        quantize_w(2, 2, 3)
-        layer(2)
-        quantize_w(3, 0, 2, "w_bf2_2")
-        term(0, 3, "w_bf3_0")
-        quantize_w(3, 2, 3)
-        layer(3)
-        term(1, 3, "w_bf3_2")
-        for d in range(D):
-            term(2, d)
+            cast_w(0, a)
+        quantize_w(0, 0)
+        gather_half(PASSES - 1, 0, "w_raw0_1")
+        quantize_w(0, 2)
+        gather_half(PASSES - 1, 1, "w_raw0_2")
+        layer(0)
+        for m in range(BLOCKS - 1):
+            for a in range(PASSES):
+                cast_w(m + 1, a)
+            early = EARLY_TERMS[m]
+            first = keep.tile([P, early, V], F32, name=f"first{m}")
+            later = keep.tile([P, D - early, V], F32, name=f"later{m}", tag=f"w_raw{m + 1}_{PASSES - 1}", align_bytes=64)
+            quantize_w(m + 1, 0)
+            for d in range(early):
+                term(m, d, first[:, d, :])
+            quantize_w(m + 1, 2)
+            layer(m + 1)
+            for d in range(early, D):
+                term(m, d, later[:, d - early, :])
+            if m > 0:
+                sum_terms(m - 1)
         m = BLOCKS - 1
+        last = keep.tile([P, D, V], F32, name="last")
         for d in range(D - 1):
-            term(m, d)
-        nc.vector.tensor_tensor(turned[m][:], terms[m, 0][:], terms[m, 1][:], ALU.add)
-        term(m, D - 1)
-        nc.vector.tensor_tensor(terms[m, 0][:], turned[m][:], terms[m, 2][:], ALU.add)
-        nc.vector.tensor_tensor(result[m][:], terms[m, 0][:], terms[m, 3][:], ALU.add)
-        for d in range(D):
-            for m in range(PAIR):
-                add_turned(m, d)
-        finish_sum(0)
-        finish_sum(1)
-        for d in range(D):
-            add_turned(2, d)
-        finish_sum(2)
-        store(3)
+            term(m, d, last[:, d, :])
+        nc.vector.tensor_tensor(partial[0][:], terms[m, 0], terms[m, 1], ALU.add)
+        term(m, D - 1, last[:, D - 1, :])
+        nc.vector.tensor_tensor(partial[1][:], partial[0][:], terms[m, 2], ALU.add)
+        nc.vector.tensor_tensor(result[m][:], partial[1][:], terms[m, 3], ALU.add)
+        sum_terms(BLOCKS - 2)
+        store(m)

@@ -21,12 +21,16 @@ PACK = 4
 K_PASS = P * PACK
 PASSES = K // K_PASS
 BLOCKS = N // P
-HALVES = V // P
+V_HALVES = V // P
+S_HALF = S // 2
+LIST_ROWS = 16
+LINE = 4
+SMALL = 8
 
 X_PIECES = [(0, 0, 512, 192), (0, 512, 512, 192), (1, 0, 512, 128), (1, 512, 512, 192),
-            (2, 0, 512, 64), (2, 512, 256, 64), (2, 768, 256, 160)]
-W_PARTS = [(0, 2), (2, 3)]
-EARLY_TERMS = [2, 1, 1]
+            (2, 0, 512, 64), (2, 512, 256, 64), (2, 768, 128, 64), (2, 896, 128, 96)]
+W_PARTS = {0: 2, 2: 3}
+TERMS_AHEAD = {(1, 0): 0, (1, 2): 1, (2, 0): 3, (2, 2): 5, (3, 0): 7, (3, 2): 8}
 
 
 def tile_picked_sub_lin_bias_sub_e_kernel(tc, xT, w, b, gate, offs, pos1, pos2, pos3, pos4, out):
@@ -35,10 +39,10 @@ def tile_picked_sub_lin_bias_sub_e_kernel(tc, xT, w, b, gate, offs, pos1, pos2, 
         keep = ctx.enter_context(tc.tile_pool(name="keep", bufs=1))
         psum = ctx.enter_context(tc.psum_pool(name="psum", bufs=1))
 
-        picked = keep.tile([P, S // 16], U16, name="picked")
-        neigh = [keep.tile([P, V // 16], U16, name=f"neigh{d}") for d in range(D)]
+        picked = keep.tile([P, S // LIST_ROWS], U16, name="picked")
+        neigh = [keep.tile([P, V // LIST_ROWS], U16, name=f"neigh{d}") for d in range(D)]
         small_rows = keep.tile([P, V], F32, name="small_rows")
-        small_cols = keep.tile([P, HALVES, 8], F32, name="small_cols")
+        small_cols = keep.tile([P, V_HALVES, SMALL], F32, name="small_cols")
         gates = keep.tile([P, D, V], F32, name="gates")
         x_raw = [keep.tile([P, PACK, n], F32, name=f"x_raw{c}") for c, (a, t0, n, nv) in enumerate(X_PIECES)]
         x_bf = [keep.tile([P, n, PACK], BF16, name=f"x_bf{c}", align_bytes=64) for c, (a, t0, n, nv) in enumerate(X_PIECES)]
@@ -50,8 +54,8 @@ def tile_picked_sub_lin_bias_sub_e_kernel(tc, xT, w, b, gate, offs, pos1, pos2, 
         for m in range(BLOCKS):
             for a in range(PASSES):
                 w_raw[m, a] = keep.tile([P, PACK, P], F32, name=f"w_raw{m}_{a}", tag=f"w_raw{m}_{a}", align_bytes=64)
-            for lo, hi in W_PARTS:
-                w_bf[m, lo] = keep.tile([P, hi - lo, P, PACK], BF16, name=f"w_bf{m}_{lo}", tag=f"w_bf{m}_{lo}", align_bytes=64)
+            for lo, hi in W_PARTS.items():
+                w_bf[m, lo] = keep.tile([P, hi - lo, P, PACK], BF16, name=f"w_bf{m}_{lo}", align_bytes=64)
                 w_words[m, lo] = keep.tile([P, hi - lo, P], U32, name=f"w_words{m}_{lo}", align_bytes=64)
                 w_bytes[m, lo] = keep.tile([P, hi - lo, P], U8, name=f"w_bytes{m}_{lo}", align_bytes=64)
         y = [keep.tile([P, S], F32, name=f"y{m}") for m in range(BLOCKS)]
@@ -69,11 +73,10 @@ def tile_picked_sub_lin_bias_sub_e_kernel(tc, xT, w, b, gate, offs, pos1, pos2, 
             rows = w[a * K_PASS : (a + 1) * K_PASS, m * P : (m + 1) * P]
             nc.sync.dma_start(out=w_raw[m, a][:], in_=rows.rearrange("(p j) n -> p j n", j=PACK))
 
-        lists = (pos1, pos2, pos3, pos4)
         nc.gpsimd.memset(small_rows[:], 0.0)
         load_x(0)
         nc.sync.dma_start(out=small_rows[0:D, :], in_=gate[:, 0, :])
-        nc.sync.dma_start(out=small_rows[D : D + 2, :], in_=b.rearrange("(e q) o -> e (q o)", e=2))
+        nc.sync.dma_start(out=small_rows[D : D + N // V, :], in_=b.rearrange("(e q) o -> e (q o)", q=V))
         nc.sync.dma_start(picked[:], offs)
         for c in range(1, len(X_PIECES)):
             load_x(c)
@@ -81,33 +84,34 @@ def tile_picked_sub_lin_bias_sub_e_kernel(tc, xT, w, b, gate, offs, pos1, pos2, 
             for a in range(PASSES):
                 load_w(m, a)
             if m == 0:
-                for d in range(D):
-                    nc.sync.dma_start(neigh[d][:], lists[d])
+                for d, places in enumerate((pos1, pos2, pos3, pos4)):
+                    nc.sync.dma_start(neigh[d][:], places)
 
         nc.gpsimd.memset(x_bytes[:], 0)
         make_identity(nc, ident[:])
-        halves = [slice(h * P, (h + 1) * P) for h in range(HALVES)]
-        cols_ps = psum.tile([P, HALVES, P], F32, name="cols_ps", tag="across0")
-        for h in range(HALVES):
-            nc.tensor.transpose(cols_ps[:, h, :], small_rows[:, halves[h]], ident[:])
-        nc.scalar.copy(small_cols[:], cols_ps[:, :, 0:8])
+
+        v_halves = [slice(h * P, (h + 1) * P) for h in range(V_HALVES)]
+        small_turned = psum.tile([P, V_HALVES, P], F32, name="small_turned", tag="across")
+        for h in range(V_HALVES):
+            nc.tensor.transpose(small_turned[:, h, :], small_rows[:, v_halves[h]], ident[:])
+        nc.scalar.copy(small_cols[:], small_turned[:, :, 0:SMALL])
         for q in range(D // 2):
             spread = psum.tile([P, 2, V], F32, name=f"spread{q}", tag=f"back{q}")
             for e in range(2):
-                for h in range(HALVES):
+                for h in range(V_HALVES):
                     column = small_cols[:, h, 2 * q + e : 2 * q + e + 1]
-                    nc.tensor.transpose(spread[:, e, halves[h]], column.to_broadcast([P, P]), ident[:])
+                    nc.tensor.transpose(spread[:, e, v_halves[h]], column.to_broadcast([P, P]), ident[:])
             nc.vector.tensor_copy(gates[:, 2 * q : 2 * q + 2, :], spread[:])
 
         def bias(m):
-            e, h = divmod(m, HALVES)
+            e, h = divmod(m, V_HALVES)
             return small_cols[:, h, D + e : D + e + 1]
 
-        def cast_x(c):
+        def round_x(c):
             a, t0, n, nv = X_PIECES[c]
             for lo, hi in ((nv, n), (0, nv)):
-                src = x_raw[c][:, :, lo:hi].rearrange("p j (c i) -> p c j i", i=4)
-                dst = x_bf[c][:, lo:hi, :].rearrange("p (c i) j -> p c j i", i=4)
+                src = x_raw[c][:, :, lo:hi].rearrange("p j (c i) -> p c j i", i=LINE)
+                dst = x_bf[c][:, lo:hi, :].rearrange("p (c i) j -> p c j i", i=LINE)
                 if lo == 0:
                     nc.vector.tensor_copy(dst, src)
                 else:
@@ -125,17 +129,21 @@ def tile_picked_sub_lin_bias_sub_e_kernel(tc, xT, w, b, gate, offs, pos1, pos2, 
             got = keep.tile([P, S], U32, name=f"got_words{a}", align_bytes=64)
             nc.vector.tensor_copy(got[:], x_words[a][:].indirect(picked[:]))
             for h in range(2):
-                got_words[a, h] = got[:, h * S // 2 : (h + 1) * S // 2]
+                got_words[a, h] = got[:, h * S_HALF : (h + 1) * S_HALF]
 
-        def gather_half(a, h, after):
-            got = keep.tile([P, S // 2], U32, name=f"got_words{a}_{h}", tag=after, align_bytes=64)
-            nc.vector.tensor_copy(got[:], x_words[a][:].indirect(picked[:, h * S // 32 : (h + 1) * S // 32]))
+        def gather_half_words(a, h, after):
+            got = keep.tile([P, S_HALF], U32, name=f"got_words{a}_{h}", tag=after, align_bytes=64)
+            entries = picked[:, h * S_HALF // LIST_ROWS : (h + 1) * S_HALF // LIST_ROWS]
+            nc.vector.tensor_copy(got[:], x_words[a][:].indirect(entries))
             got_words[a, h] = got[:]
 
-        def cast_w(m, a):
-            src = w_raw[m, a][:].rearrange("p j (c i) -> p c j i", i=4)
-            lo = max(first for first, end in W_PARTS if first <= a)
-            dst = w_bf[m, lo][:, a - lo, :, :].rearrange("p (c i) j -> p c j i", i=4)
+        def part_of(a):
+            return max(lo for lo in W_PARTS if lo <= a)
+
+        def round_w(m, a):
+            lo = part_of(a)
+            src = w_raw[m, a][:].rearrange("p j (c i) -> p c j i", i=LINE)
+            dst = w_bf[m, lo][:, a - lo, :, :].rearrange("p (c i) j -> p c j i", i=LINE)
             nc.scalar.activation(dst, src, ACT.Copy)
 
         def quantize_w(m, lo):
@@ -146,47 +154,48 @@ def tile_picked_sub_lin_bias_sub_e_kernel(tc, xT, w, b, gate, offs, pos1, pos2, 
             )
 
         def layer(m):
-            n = S // 2
-            accs = [psum.tile([P, n], F32, name=f"acc{m}_{h}", tag=f"acc{m % 2}_{h}") for h in range(2)]
+            accs = [psum.tile([P, S_HALF], F32, name=f"acc{m}_{h}", tag=f"acc{m % 2}_{h}") for h in range(2)]
             for a in range(PASSES):
-                lo = max(first for first, end in W_PARTS if first <= a)
+                lo = part_of(a)
                 for h in range(2):
-                    cols = slice(h * n, (h + 1) * n)
                     nc.tensor.matmul_mx(
                         out=accs[h][:],
                         lhsT=w_words[m, lo][:, a - lo, :].bitcast(FP8X4),
                         lhsT_scale=w_bytes[m, lo][:, a - lo, :],
                         rhs=got_words[a, h].bitcast(FP8X4),
-                        rhs_scale=got_bytes[PACK * a :, cols],
+                        rhs_scale=got_bytes[PACK * a :, h * S_HALF : (h + 1) * S_HALF],
                         start=(a == 0),
                         stop=(a == PASSES - 1),
                     )
             for h in range(2):
-                nc.scalar.activation(y[m][:, h * n : (h + 1) * n], accs[h][:], ACT.Identity, bias=bias(m))
+                picked_half = y[m][:, h * S_HALF : (h + 1) * S_HALF]
+                if m == 0:
+                    nc.vector.tensor_scalar_add(picked_half, accs[h][:], bias(m))
+                else:
+                    nc.scalar.activation(picked_half, accs[h][:], ACT.Identity, bias=bias(m))
 
         def term(m, d, dst):
             terms[m, d] = dst
             nc.vector.tensor_tensor(dst, y[m][:].indirect(neigh[d][:]), gates[:, d, :], ALU.mult)
 
+        def store(m):
+            nc.sync.dma_start(out=out[m * P : (m + 1) * P, :], in_=result[m][:])
+
         def sum_terms(m):
-            across = psum.tile([P, V], F32, name=f"across{m}", tag="across0")
-            for cols in halves:
+            across = psum.tile([P, V], F32, name=f"across{m}", tag=f"acc{m % 2}_0" if m + 2 < BLOCKS else "across")
+            for cols in v_halves:
                 for d in range(D):
                     nc.tensor.matmul(across[:, cols], terms[m, d][:, cols], ident[:], start=(d == 0), stop=(d == D - 1), is_transpose=True)
-            hold = f"w_bf{m + 2}_{PASSES - 1}" if m + 2 < BLOCKS else f"turned{m}"
-            turned = keep.tile([P, V], F32, name=f"turned{m}", tag=hold, align_bytes=64)
+            turned = keep.tile([P, V], F32, name=f"turned{m}")
             nc.scalar.copy(turned[:], across[:])
             back = psum.tile([P, V], F32, name=f"back{m}", tag=f"back{m % 2}")
-            for cols in halves:
+            for cols in v_halves:
                 nc.tensor.transpose(back[:, cols], turned[:, cols], ident[:])
             nc.scalar.copy(result[m][:], back[:])
             store(m)
 
-        def store(m):
-            nc.sync.dma_start(out=out[m * P : (m + 1) * P, :], in_=result[m][:])
-
         for c in range(len(X_PIECES)):
-            cast_x(c)
+            round_x(c)
             if c > 0:
                 quantize_x(c - 1)
                 before, now = X_PIECES[c - 1][0], X_PIECES[c][0]
@@ -194,35 +203,38 @@ def tile_picked_sub_lin_bias_sub_e_kernel(tc, xT, w, b, gate, offs, pos1, pos2, 
                     gather_words(before)
         quantize_x(len(X_PIECES) - 1)
         nc.vector.tensor_copy(got_bytes[:], x_bytes[:].indirect(picked[:]))
+
         for a in range(PASSES):
-            cast_w(0, a)
-        quantize_w(0, 0)
-        gather_half(PASSES - 1, 0, "w_raw0_1")
-        quantize_w(0, 2)
-        gather_half(PASSES - 1, 1, "w_raw0_2")
+            round_w(0, a)
+        for h, (lo, hi) in enumerate(W_PARTS.items()):
+            quantize_w(0, lo)
+            gather_half_words(PASSES - 1, h, after=f"w_raw0_{hi - 1}")
         layer(0)
-        for m in range(BLOCKS - 1):
-            for a in range(PASSES):
-                cast_w(m + 1, a)
-            early = EARLY_TERMS[m]
-            first = keep.tile([P, early, V], F32, name=f"first{m}")
-            later = keep.tile([P, D - early, V], F32, name=f"later{m}", tag=f"w_raw{m + 1}_{PASSES - 1}", align_bytes=64)
-            quantize_w(m + 1, 0)
-            for d in range(early):
-                term(m, d, first[:, d, :])
-            quantize_w(m + 1, 2)
-            layer(m + 1)
-            for d in range(early, D):
-                term(m, d, later[:, d - early, :])
-            if m > 0:
-                sum_terms(m - 1)
-        m = BLOCKS - 1
-        last = keep.tile([P, D, V], F32, name="last")
+
+        early_terms = (BLOCKS - 1) * D
+        calls = {ahead: call for call, ahead in TERMS_AHEAD.items()}
+        starts = sorted(calls) + [early_terms]
+        for first, end in zip(starts, starts[1:]):
+            m, lo = calls[first]
+            hi = W_PARTS[lo]
+            for a in range(lo, hi):
+                round_w(m, a)
+            quantize_w(m, lo)
+            if hi == PASSES:
+                layer(m)
+            run = keep.tile([P, end - first, V], F32, name=f"run{first}", tag=f"w_raw{m}_{hi - 1}", align_bytes=64)
+            for i in range(first, end):
+                term(i // D, i % D, run[:, i - first, :])
+        for m in range(BLOCKS - 2):
+            sum_terms(m)
+
+        last = BLOCKS - 1
+        last_terms = keep.tile([P, D, V], F32, name="last_terms")
         for d in range(D - 1):
-            term(m, d, last[:, d, :])
-        nc.vector.tensor_tensor(partial[0][:], terms[m, 0], terms[m, 1], ALU.add)
-        term(m, D - 1, last[:, D - 1, :])
-        nc.vector.tensor_tensor(partial[1][:], partial[0][:], terms[m, 2], ALU.add)
-        nc.vector.tensor_tensor(result[m][:], partial[1][:], terms[m, 3], ALU.add)
+            term(last, d, last_terms[:, d, :])
+        nc.vector.tensor_tensor(partial[0][:], terms[last, 0], terms[last, 1], ALU.add)
+        term(last, D - 1, last_terms[:, D - 1, :])
+        nc.vector.tensor_tensor(partial[1][:], partial[0][:], terms[last, 2], ALU.add)
+        nc.vector.tensor_tensor(result[last][:], partial[1][:], terms[last, 3], ALU.add)
         sum_terms(BLOCKS - 2)
-        store(m)
+        store(last)

@@ -27,8 +27,9 @@ LIST_ROWS = 16
 LINE = 4
 SMALL = 8
 
-X_PIECES = [(0, 0, 512, 192), (0, 512, 512, 192), (1, 0, 512, 128), (1, 512, 512, 192),
-            (2, 0, 512, 64), (2, 512, 256, 64), (2, 768, 128, 64), (2, 896, 128, 96)]
+X_LOADS = [(0, 0, T), (1, 0, T), (2, 0, 512), (2, 512, 256), (2, 768, 256)]
+X_PIECES = [(0, 0, 512, 512), (0, 512, 512, 128), (1, 0, 512, 512), (1, 512, 512, 64),
+            (2, 0, 512, 128), (2, 512, 256, 64), (2, 768, 256, 96)]
 W_PARTS = {0: 2, 2: 3}
 TERMS_AHEAD = {(1, 0): 0, (1, 2): 1, (2, 0): 3, (2, 2): 5, (3, 0): 7, (3, 2): 8}
 
@@ -43,8 +44,7 @@ def tile_picked_sub_lin_bias_sub_e_kernel(tc, xT, w, b, gate, offs, pos1, pos2, 
         neigh = [keep.tile([P, V // LIST_ROWS], U16, name=f"neigh{d}") for d in range(D)]
         small_rows = keep.tile([P, V], F32, name="small_rows")
         small_cols = keep.tile([P, V_HALVES, SMALL], F32, name="small_cols")
-        gates = keep.tile([P, D, V], F32, name="gates")
-        x_raw = [keep.tile([P, PACK, n], F32, name=f"x_raw{c}") for c, (a, t0, n, nv) in enumerate(X_PIECES)]
+        x_raw = [keep.tile([P, PACK, n], F32, name=f"x_raw{c}", tag=f"x_raw{c}") for c, (a, t0, n) in enumerate(X_LOADS)]
         x_bf = [keep.tile([P, n, PACK], BF16, name=f"x_bf{c}", align_bytes=64) for c, (a, t0, n, nv) in enumerate(X_PIECES)]
         x_words = [keep.tile([P, T], U32, name=f"x_words{a}", align_bytes=64) for a in range(PASSES)]
         x_bytes = keep.tile([P, T], U8, name="x_bytes", align_bytes=64)
@@ -64,21 +64,21 @@ def tile_picked_sub_lin_bias_sub_e_kernel(tc, xT, w, b, gate, offs, pos1, pos2, 
         partial = [keep.tile([P, V], F32, name=f"partial{i}") for i in range(2)]
         ident = keep.tile([P, P], F32, name="ident")
 
-        def load_x(c):
-            a, t0, n, nv = X_PIECES[c]
+        def load_x(c, j0=0, j1=PACK):
+            a, t0, n = X_LOADS[c]
             rows = xT[a * K_PASS : (a + 1) * K_PASS, t0 : t0 + n]
-            nc.sync.dma_start(out=x_raw[c][:], in_=rows.rearrange("(p j) t -> p j t", j=PACK))
+            nc.sync.dma_start(out=x_raw[c][:, j0:j1, :], in_=rows.rearrange("(p j) t -> p j t", j=PACK)[:, j0:j1, :])
 
         def load_w(m, a):
             rows = w[a * K_PASS : (a + 1) * K_PASS, m * P : (m + 1) * P]
             nc.sync.dma_start(out=w_raw[m, a][:], in_=rows.rearrange("(p j) n -> p j n", j=PACK))
 
-        nc.gpsimd.memset(small_rows[:], 0.0)
+        nc.vector.memset(small_rows[:], 0.0)
         load_x(0)
         nc.sync.dma_start(out=small_rows[0:D, :], in_=gate[:, 0, :])
         nc.sync.dma_start(out=small_rows[D : D + N // V, :], in_=b.rearrange("(e q) o -> e (q o)", q=V))
         nc.sync.dma_start(picked[:], offs)
-        for c in range(1, len(X_PIECES)):
+        for c in range(1, len(X_LOADS)):
             load_x(c)
         for m in range(BLOCKS):
             for a in range(PASSES):
@@ -87,21 +87,22 @@ def tile_picked_sub_lin_bias_sub_e_kernel(tc, xT, w, b, gate, offs, pos1, pos2, 
                 for d, places in enumerate((pos1, pos2, pos3, pos4)):
                     nc.sync.dma_start(neigh[d][:], places)
 
-        nc.gpsimd.memset(x_bytes[:], 0)
+        nc.vector.memset(x_bytes[:].bitcast(U32), 0)
         make_identity(nc, ident[:])
 
         v_halves = [slice(h * P, (h + 1) * P) for h in range(V_HALVES)]
         small_turned = psum.tile([P, V_HALVES, P], F32, name="small_turned", tag="across")
         for h in range(V_HALVES):
             nc.tensor.transpose(small_turned[:, h, :], small_rows[:, v_halves[h]], ident[:])
-        nc.scalar.copy(small_cols[:], small_turned[:, :, 0:SMALL])
+        nc.vector.tensor_copy(small_cols[:], small_turned[:, :, 0:SMALL])
+        spreads = []
         for q in range(D // 2):
             spread = psum.tile([P, 2, V], F32, name=f"spread{q}", tag=f"back{q}")
             for e in range(2):
                 for h in range(V_HALVES):
                     column = small_cols[:, h, 2 * q + e : 2 * q + e + 1]
                     nc.tensor.transpose(spread[:, e, v_halves[h]], column.to_broadcast([P, P]), ident[:])
-            nc.vector.tensor_copy(gates[:, 2 * q : 2 * q + 2, :], spread[:])
+            spreads.append(spread)
 
         def bias(m):
             e, h = divmod(m, V_HALVES)
@@ -109,8 +110,12 @@ def tile_picked_sub_lin_bias_sub_e_kernel(tc, xT, w, b, gate, offs, pos1, pos2, 
 
         def round_x(c):
             a, t0, n, nv = X_PIECES[c]
+            load = max(i for i, (b0, s0, n0) in enumerate(X_LOADS) if (b0, s0) <= (a, t0))
+            skip = t0 - X_LOADS[load][1]
             for lo, hi in ((nv, n), (0, nv)):
-                src = x_raw[c][:, :, lo:hi].rearrange("p j (c i) -> p c j i", i=LINE)
+                if lo == hi:
+                    continue
+                src = x_raw[load][:, :, skip + lo : skip + hi].rearrange("p j (c i) -> p c j i", i=LINE)
                 dst = x_bf[c][:, lo:hi, :].rearrange("p (c i) j -> p c j i", i=LINE)
                 if lo == 0:
                     nc.vector.tensor_copy(dst, src)
@@ -196,6 +201,10 @@ def tile_picked_sub_lin_bias_sub_e_kernel(tc, xT, w, b, gate, offs, pos1, pos2, 
 
         for c in range(len(X_PIECES)):
             round_x(c)
+            if c == 1:
+                gates = keep.tile([P, D, V], F32, name="gates", tag="x_raw0")
+                for q in range(D // 2):
+                    nc.scalar.copy(gates[:, 2 * q : 2 * q + 2, :], spreads[q][:])
             if c > 0:
                 quantize_x(c - 1)
                 before, now = X_PIECES[c - 1][0], X_PIECES[c][0]

@@ -31,13 +31,14 @@ X_LOADS = [(0, 0, T), (1, 0, T), (2, 0, 512), (2, 512, 256), (2, 768, 256)]
 X_PIECES = [(0, 0, 512, 512), (0, 512, 512, 128), (1, 0, 512, 512), (1, 512, 512, 64),
             (2, 0, 512, 128), (2, 512, 256, 64), (2, 768, 256, 96)]
 W_PARTS = {0: 2, 2: 3}
-TERMS_AHEAD = {(1, 0): 0, (1, 2): 1, (2, 0): 3, (2, 2): 5, (3, 0): 7, (3, 2): 8}
+TERMS_AHEAD = {(1, 0): 0, (1, 2): 2, (2, 0): 3, (2, 2): 5, (3, 0): 7, (3, 2): 8}
 
 
 def tile_picked_sub_lin_bias_sub_e_kernel(tc, xT, w, b, gate, offs, pos1, pos2, pos3, pos4, out):
     nc = tc.nc
     with ExitStack() as ctx:
         keep = ctx.enter_context(tc.tile_pool(name="keep", bufs=1))
+        placed = ctx.enter_context(tc.tile_pool(name="placed", bufs=1))
         psum = ctx.enter_context(tc.psum_pool(name="psum", bufs=1))
 
         picked = keep.tile([P, S // LIST_ROWS], U16, name="picked")
@@ -53,15 +54,18 @@ def tile_picked_sub_lin_bias_sub_e_kernel(tc, xT, w, b, gate, offs, pos1, pos2, 
         w_raw, w_bf, w_words, w_bytes = {}, {}, {}, {}
         for m in range(BLOCKS):
             for a in range(PASSES):
-                w_raw[m, a] = keep.tile([P, PACK, P], F32, name=f"w_raw{m}_{a}", tag=f"w_raw{m}_{a}", align_bytes=64)
+                if (m, a) == (1, 1):
+                    w_raw[m, a] = placed.tile([P, PACK, P], F32, name="w_raw1_1", offset=0, align_bytes=64)
+                else:
+                    w_raw[m, a] = keep.tile([P, PACK, P], F32, name=f"w_raw{m}_{a}", tag=f"w_raw{m}_{a}", align_bytes=64)
             for lo, hi in W_PARTS.items():
-                w_bf[m, lo] = keep.tile([P, hi - lo, P, PACK], BF16, name=f"w_bf{m}_{lo}", align_bytes=64)
+                if (m, hi) != (1, PASSES):
+                    w_bf[m, lo] = keep.tile([P, hi - lo, P, PACK], BF16, name=f"w_bf{m}_{lo}", align_bytes=64)
                 w_words[m, lo] = keep.tile([P, hi - lo, P], U32, name=f"w_words{m}_{lo}", align_bytes=64)
                 w_bytes[m, lo] = keep.tile([P, hi - lo, P], U8, name=f"w_bytes{m}_{lo}", align_bytes=64)
         y = [keep.tile([P, S], F32, name=f"y{m}") for m in range(BLOCKS)]
         terms = {}
         result = [keep.tile([P, V], F32, name=f"result{m}") for m in range(BLOCKS)]
-        partial = [keep.tile([P, V], F32, name=f"partial{i}") for i in range(2)]
         ident = keep.tile([P, P], F32, name="ident")
 
         def load_x(c, j0=0, j1=PACK):
@@ -83,9 +87,9 @@ def tile_picked_sub_lin_bias_sub_e_kernel(tc, xT, w, b, gate, offs, pos1, pos2, 
         for m in range(BLOCKS):
             for a in range(PASSES):
                 load_w(m, a)
-            if m == 0:
-                for d, places in enumerate((pos1, pos2, pos3, pos4)):
-                    nc.sync.dma_start(neigh[d][:], places)
+                if (m, a) == (1, 1):
+                    for d, places in enumerate((pos1, pos2, pos3, pos4)):
+                        nc.sync.dma_start(neigh[d][:], places)
 
         nc.vector.memset(x_bytes[:].bitcast(U32), 0)
         make_identity(nc, ident[:])
@@ -95,6 +99,8 @@ def tile_picked_sub_lin_bias_sub_e_kernel(tc, xT, w, b, gate, offs, pos1, pos2, 
         for h in range(V_HALVES):
             nc.tensor.transpose(small_turned[:, h, :], small_rows[:, v_halves[h]], ident[:])
         nc.vector.tensor_copy(small_cols[:], small_turned[:, :, 0:SMALL])
+        last_cols = keep.tile([P, SMALL], F32, name="last_cols", tag="last_cols")
+        nc.vector.tensor_copy(last_cols[:], small_turned[:, (BLOCKS - 1) % V_HALVES, 0:SMALL])
         spreads = []
         for q in range(D // 2):
             spread = psum.tile([P, 2, V], F32, name=f"spread{q}", tag=f"back{q}")
@@ -106,6 +112,8 @@ def tile_picked_sub_lin_bias_sub_e_kernel(tc, xT, w, b, gate, offs, pos1, pos2, 
 
         def bias(m):
             e, h = divmod(m, V_HALVES)
+            if m == BLOCKS - 1:
+                return last_cols[:, D + e : D + e + 1]
             return small_cols[:, h, D + e : D + e + 1]
 
         def round_x(c):
@@ -174,8 +182,10 @@ def tile_picked_sub_lin_bias_sub_e_kernel(tc, xT, w, b, gate, offs, pos1, pos2, 
                     )
             for h in range(2):
                 picked_half = y[m][:, h * S_HALF : (h + 1) * S_HALF]
-                if m == 0:
+                if (m, h) == (0, 0):
                     nc.vector.tensor_scalar_add(picked_half, accs[h][:], bias(m))
+                elif m == 0:
+                    nc.scalar.activation(picked_half, accs[h][:], ACT.Identity, bias=first_cols[:, D : D + 1])
                 else:
                     nc.scalar.activation(picked_half, accs[h][:], ACT.Identity, bias=bias(m))
 
@@ -187,12 +197,12 @@ def tile_picked_sub_lin_bias_sub_e_kernel(tc, xT, w, b, gate, offs, pos1, pos2, 
             nc.sync.dma_start(out=out[m * P : (m + 1) * P, :], in_=result[m][:])
 
         def sum_terms(m):
-            across = psum.tile([P, V], F32, name=f"across{m}", tag=f"acc{m % 2}_0" if m + 2 < BLOCKS else "across")
+            across = psum.tile([P, V], F32, name=f"across{m}", tag="across" if m == 0 else f"acc{m % 2}_0")
             for cols in v_halves:
                 for d in range(D):
                     nc.tensor.matmul(across[:, cols], terms[m, d][:, cols], ident[:], start=(d == 0), stop=(d == D - 1), is_transpose=True)
-            turned = keep.tile([P, V], F32, name=f"turned{m}")
-            nc.scalar.copy(turned[:], across[:])
+            turned = spare[:, m, :]
+            nc.scalar.copy(turned, across[:])
             back = psum.tile([P, V], F32, name=f"back{m}", tag=f"back{m % 2}")
             for cols in v_halves:
                 nc.tensor.transpose(back[:, cols], turned[:, cols], ident[:])
@@ -218,32 +228,55 @@ def tile_picked_sub_lin_bias_sub_e_kernel(tc, xT, w, b, gate, offs, pos1, pos2, 
         for h, (lo, hi) in enumerate(W_PARTS.items()):
             quantize_w(0, lo)
             gather_half_words(PASSES - 1, h, after=f"w_raw0_{hi - 1}")
+        for a in range(W_PARTS[0]):
+            round_w(1, a)
+        first_cols = placed.tile([P, SMALL], F32, name="first_cols", offset=0, align_bytes=64)
+        nc.scalar.copy(first_cols[:], small_cols[:, 0, :])
         layer(0)
 
-        early_terms = (BLOCKS - 1) * D
+        early_terms = (BLOCKS - 1) * D - 1
         calls = {ahead: call for call, ahead in TERMS_AHEAD.items()}
         starts = sorted(calls) + [early_terms]
         for first, end in zip(starts, starts[1:]):
             m, lo = calls[first]
             hi = W_PARTS[lo]
+            if (m, hi) == (1, PASSES):
+                w_bf[m, lo] = placed.tile([P, hi - lo, P, PACK], BF16, name=f"w_bf{m}_{lo}", offset=0, align_bytes=64)
             for a in range(lo, hi):
-                round_w(m, a)
+                if first > 0:
+                    round_w(m, a)
             quantize_w(m, lo)
             if hi == PASSES:
                 layer(m)
-            run = keep.tile([P, end - first, V], F32, name=f"run{first}", tag=f"w_raw{m}_{hi - 1}", align_bytes=64)
+            if first == 0:
+                run = placed.tile([P, end - first, V], F32, name="run0", offset=4 * V, align_bytes=64)
+            else:
+                run = keep.tile([P, end - first + (BLOCKS - 2 if end == early_terms else 0), V], F32, name=f"run{first}", tag=f"w_raw{m}_{hi - 1}", align_bytes=64)
+            spare = run[:, end - first :, :]
             for i in range(first, end):
                 term(i // D, i % D, run[:, i - first, :])
         for m in range(BLOCKS - 2):
             sum_terms(m)
 
         last = BLOCKS - 1
-        last_terms = keep.tile([P, D, V], F32, name="last_terms")
+        last_terms = keep.tile([P, D + 1, V], F32, name="last_terms", tag="last_cols")
         for d in range(D - 1):
             term(last, d, last_terms[:, d, :])
-        nc.vector.tensor_tensor(partial[0][:], terms[last, 0], terms[last, 1], ALU.add)
+        term(last - 1, D - 1, last_terms[:, D, :])
         term(last, D - 1, last_terms[:, D - 1, :])
-        nc.vector.tensor_tensor(partial[1][:], partial[0][:], terms[last, 2], ALU.add)
-        nc.vector.tensor_tensor(result[last][:], partial[1][:], terms[last, 3], ALU.add)
-        sum_terms(BLOCKS - 2)
-        store(last)
+        whole = psum.tile([P, V], F32, name="across_whole", tag="across")
+        banks = {last - 1: [whole[:, cols] for cols in v_halves],
+                 last: [psum.tile([P, P], F32, name=f"across_half{h}", tag=f"acc0_{h}")[:] for h in range(V_HALVES)]}
+        steps = {last - 1: [(h, d) for h in range(V_HALVES) for d in range(D - 1)],
+                 last: [(h, d) for d in range(D - 1) for h in range(V_HALVES)]}
+        for m in (last - 1, last):
+            for h, d in steps[m]:
+                nc.tensor.matmul(banks[m][h], terms[m, d][:, v_halves[h]], ident[:], start=(d == 0), stop=(d == D - 2), is_transpose=True)
+            turned = keep.tile([P, V], F32, name=f"turned{m}")
+            back = psum.tile([P, V], F32, name=f"back{m}", tag=f"back{m % 2}")
+            for h, cols in enumerate(v_halves):
+                nc.scalar.copy(turned[:, cols], banks[m][h])
+            for cols in v_halves:
+                nc.tensor.transpose(back[:, cols], turned[:, cols], ident[:])
+            nc.vector.tensor_tensor(result[m][:], back[:], terms[m, D - 1], ALU.add)
+            store(m)

@@ -23,15 +23,16 @@ PASSES = K // K_PASS
 BLOCKS = N // P
 V_HALVES = V // P
 S_HALF = S // 2
+FIRST_GROUPS = [(0, S_HALF), (S_HALF, S_HALF // 2), (3 * S_HALF // 2, S_HALF // 2)]
 LIST_ROWS = 16
 LINE = 4
 SMALL = 8
 
 X_LOADS = [(0, 0, T), (1, 0, T), (2, 0, 512), (2, 512, 256), (2, 768, 256)]
 X_PIECES = [(0, 0, 512, 512), (0, 512, 512, 128), (1, 0, 512, 512), (1, 512, 512, 64),
-            (2, 0, 512, 128), (2, 512, 256, 64), (2, 768, 256, 96)]
+            (2, 0, 512, 128), (2, 512, 256, 64), (2, 768, 128, 128), (2, 896, 128, 0)]
 W_PARTS = {0: 2, 2: 3}
-TERMS_AHEAD = {(1, 0): 0, (1, 2): 2, (2, 0): 3, (2, 2): 5, (3, 0): 7, (3, 2): 8}
+TERMS_AHEAD = {(1, 0): 0, (1, 2): 2, (2, 0): 4, (2, 2): 5, (3, 0): 7, (3, 2): 8}
 
 
 def tile_picked_sub_lin_bias_sub_e_kernel(tc, xT, w, b, gate, offs, pos1, pos2, pos3, pos4, out):
@@ -125,7 +126,7 @@ def tile_picked_sub_lin_bias_sub_e_kernel(tc, xT, w, b, gate, offs, pos1, pos2, 
                     continue
                 src = x_raw[load][:, :, skip + lo : skip + hi].rearrange("p j (c i) -> p c j i", i=LINE)
                 dst = x_bf[c][:, lo:hi, :].rearrange("p (c i) j -> p c j i", i=LINE)
-                if lo == 0:
+                if hi == nv and lo == 0:
                     nc.vector.tensor_copy(dst, src)
                 else:
                     nc.scalar.activation(dst, src, ACT.Copy)
@@ -146,8 +147,10 @@ def tile_picked_sub_lin_bias_sub_e_kernel(tc, xT, w, b, gate, offs, pos1, pos2, 
 
         def gather_half_words(a, h, after):
             got = keep.tile([P, S_HALF], U32, name=f"got_words{a}_{h}", tag=after, align_bytes=64)
-            entries = picked[:, h * S_HALF // LIST_ROWS : (h + 1) * S_HALF // LIST_ROWS]
-            nc.vector.tensor_copy(got[:], x_words[a][:].indirect(entries))
+            for first, count in FIRST_GROUPS:
+                if first // S_HALF == h:
+                    entries = picked[:, first // LIST_ROWS : (first + count) // LIST_ROWS]
+                    nc.vector.tensor_copy(got[:, first % S_HALF : first % S_HALF + count], x_words[a][:].indirect(entries))
             got_words[a, h] = got[:]
 
         def part_of(a):
@@ -167,21 +170,22 @@ def tile_picked_sub_lin_bias_sub_e_kernel(tc, xT, w, b, gate, offs, pos1, pos2, 
             )
 
         def layer(m):
-            accs = [psum.tile([P, S_HALF], F32, name=f"acc{m}_{h}", tag=f"acc{m % 2}_{h}") for h in range(2)]
+            groups = FIRST_GROUPS if m == 0 else [(0, S_HALF), (S_HALF, S_HALF)]
+            accs = [psum.tile([P, n], F32, name=f"acc{m}_{h}", tag=f"acc{m % 2}_{h}") for h, (first, n) in enumerate(groups)]
             for a in range(PASSES):
                 lo = part_of(a)
-                for h in range(2):
+                for h, (first, n) in enumerate(groups):
                     nc.tensor.matmul_mx(
                         out=accs[h][:],
                         lhsT=w_words[m, lo][:, a - lo, :].bitcast(FP8X4),
                         lhsT_scale=w_bytes[m, lo][:, a - lo, :],
-                        rhs=got_words[a, h].bitcast(FP8X4),
-                        rhs_scale=got_bytes[PACK * a :, h * S_HALF : (h + 1) * S_HALF],
+                        rhs=got_words[a, first // S_HALF][:, first % S_HALF : first % S_HALF + n].bitcast(FP8X4),
+                        rhs_scale=got_bytes[PACK * a :, first : first + n],
                         start=(a == 0),
                         stop=(a == PASSES - 1),
                     )
-            for h in range(2):
-                picked_half = y[m][:, h * S_HALF : (h + 1) * S_HALF]
+            for h, (first, n) in enumerate(groups):
+                picked_half = y[m][:, first : first + n]
                 if (m, h) == (0, 0):
                     nc.vector.tensor_scalar_add(picked_half, accs[h][:], bias(m))
                 elif m == 0:

@@ -26,11 +26,11 @@ S_HALF = S // 2
 FIRST_GROUPS = [(0, S_HALF), (S_HALF, S_HALF // 2), (3 * S_HALF // 2, S_HALF // 2)]
 LIST_ROWS = 16
 LINE = 4
-SMALL = 8
+RUN = D * V // P
 
 X_LOADS = [(0, 0, T), (1, 0, T), (2, 0, 512), (2, 512, 256), (2, 768, 256)]
-X_PIECES = [(0, 0, 512, 512), (0, 512, 512, 128), (1, 0, 512, 512), (1, 512, 512, 64),
-            (2, 0, 512, 128), (2, 512, 256, 64), (2, 768, 128, 128), (2, 896, 128, 0)]
+X_PIECES = [(0, 0, 512, 512), (0, 512, 512, 64), (1, 0, 512, 512), (1, 512, 512, 64),
+            (2, 0, 512, 128), (2, 512, 256, 0), (2, 768, 256, 160)]
 W_PARTS = {0: 2, 2: 3}
 TERMS_AHEAD = {(1, 0): 0, (1, 2): 2, (2, 0): 4, (2, 2): 5, (3, 0): 7, (3, 2): 8}
 
@@ -44,11 +44,11 @@ def tile_picked_sub_lin_bias_sub_e_kernel(tc, xT, w, b, gate, offs, pos1, pos2, 
 
         picked = keep.tile([P, S // LIST_ROWS], U16, name="picked")
         neigh = [keep.tile([P, V // LIST_ROWS], U16, name=f"neigh{d}") for d in range(D)]
-        small_rows = keep.tile([P, V], F32, name="small_rows")
-        small_cols = keep.tile([P, V_HALVES, SMALL], F32, name="small_cols")
+        gate_runs = keep.tile([P, RUN], F32, name="gate_runs")
+        bias_rows = keep.tile([P, P], F32, name="bias_rows")
         x_raw = [keep.tile([P, PACK, n], F32, name=f"x_raw{c}", tag=f"x_raw{c}") for c, (a, t0, n) in enumerate(X_LOADS)]
-        x_bf = [keep.tile([P, n, PACK], BF16, name=f"x_bf{c}", align_bytes=64) for c, (a, t0, n, nv) in enumerate(X_PIECES)]
-        x_words = [keep.tile([P, T], U32, name=f"x_words{a}", align_bytes=64) for a in range(PASSES)]
+        x_bf = [keep.tile([P, n, PACK], BF16, name=f"x_bf{c}", tag=f"x_bf{c}", align_bytes=64) for c, (a, t0, n, nv) in enumerate(X_PIECES)]
+        x_words = [keep.tile([P, T], U32, name=f"x_words{a}", tag=f"x_words{a}", align_bytes=64) for a in range(PASSES)]
         x_bytes = keep.tile([P, T], U8, name="x_bytes", align_bytes=64)
         got_words = {}
         got_bytes = keep.tile([P, S], U8, name="got_bytes", align_bytes=64)
@@ -69,19 +69,19 @@ def tile_picked_sub_lin_bias_sub_e_kernel(tc, xT, w, b, gate, offs, pos1, pos2, 
         result = [keep.tile([P, V], F32, name=f"result{m}") for m in range(BLOCKS)]
         ident = keep.tile([P, P], F32, name="ident")
 
-        def load_x(c, j0=0, j1=PACK):
+        def load_x(c):
             a, t0, n = X_LOADS[c]
             rows = xT[a * K_PASS : (a + 1) * K_PASS, t0 : t0 + n]
-            nc.sync.dma_start(out=x_raw[c][:, j0:j1, :], in_=rows.rearrange("(p j) t -> p j t", j=PACK)[:, j0:j1, :])
+            nc.sync.dma_start(out=x_raw[c][:], in_=rows.rearrange("(p j) t -> p j t", j=PACK))
 
         def load_w(m, a):
             rows = w[a * K_PASS : (a + 1) * K_PASS, m * P : (m + 1) * P]
             nc.sync.dma_start(out=w_raw[m, a][:], in_=rows.rearrange("(p j) n -> p j n", j=PACK))
 
-        nc.vector.memset(small_rows[:], 0.0)
+        nc.vector.memset(bias_rows[:], 0.0)
         load_x(0)
-        nc.sync.dma_start(out=small_rows[0:D, :], in_=gate[:, 0, :])
-        nc.sync.dma_start(out=small_rows[D : D + N // V, :], in_=b.rearrange("(e q) o -> e (q o)", q=V))
+        nc.sync.dma_start(out=gate_runs[:], in_=gate[:, 0, :].rearrange("d (q i) -> d q i", i=RUN))
+        nc.sync.dma_start(out=bias_rows[0:BLOCKS, :], in_=b.rearrange("(m q) o -> m (q o)", q=P))
         nc.sync.dma_start(picked[:], offs)
         for c in range(1, len(X_LOADS)):
             load_x(c)
@@ -96,26 +96,15 @@ def tile_picked_sub_lin_bias_sub_e_kernel(tc, xT, w, b, gate, offs, pos1, pos2, 
         make_identity(nc, ident[:])
 
         v_halves = [slice(h * P, (h + 1) * P) for h in range(V_HALVES)]
-        small_turned = psum.tile([P, V_HALVES, P], F32, name="small_turned", tag="across")
-        for h in range(V_HALVES):
-            nc.tensor.transpose(small_turned[:, h, :], small_rows[:, v_halves[h]], ident[:])
-        nc.vector.tensor_copy(small_cols[:], small_turned[:, :, 0:SMALL])
-        last_cols = keep.tile([P, SMALL], F32, name="last_cols", tag="last_cols")
-        nc.vector.tensor_copy(last_cols[:], small_turned[:, (BLOCKS - 1) % V_HALVES, 0:SMALL])
         spreads = []
-        for q in range(D // 2):
-            spread = psum.tile([P, 2, V], F32, name=f"spread{q}", tag=f"back{q}")
-            for e in range(2):
-                for h in range(V_HALVES):
-                    column = small_cols[:, h, 2 * q + e : 2 * q + e + 1]
-                    nc.tensor.transpose(spread[:, e, v_halves[h]], column.to_broadcast([P, P]), ident[:])
-            spreads.append(spread)
+        for e in range(RUN // LINE):
+            spreads.append(psum.tile([P, LINE, P], F32, name=f"spread{e}", tag=f"back{e}"))
+            for i in range(LINE):
+                column = gate_runs[:, e * LINE + i : e * LINE + i + 1]
+                nc.tensor.transpose(spreads[e][:, i, :], column.to_broadcast([P, P]), ident[:])
 
         def bias(m):
-            e, h = divmod(m, V_HALVES)
-            if m == BLOCKS - 1:
-                return last_cols[:, D + e : D + e + 1]
-            return small_cols[:, h, D + e : D + e + 1]
+            return bias_cols[:, m : m + 1]
 
         def round_x(c):
             a, t0, n, nv = X_PIECES[c]
@@ -189,7 +178,7 @@ def tile_picked_sub_lin_bias_sub_e_kernel(tc, xT, w, b, gate, offs, pos1, pos2, 
                 if (m, h) == (0, 0):
                     nc.vector.tensor_scalar_add(picked_half, accs[h][:], bias(m))
                 elif m == 0:
-                    nc.scalar.activation(picked_half, accs[h][:], ACT.Identity, bias=first_cols[:, D : D + 1])
+                    nc.scalar.activation(picked_half, accs[h][:], ACT.Identity, bias=first_cols[:, 0:1])
                 else:
                     nc.scalar.activation(picked_half, accs[h][:], ACT.Identity, bias=bias(m))
 
@@ -217,14 +206,19 @@ def tile_picked_sub_lin_bias_sub_e_kernel(tc, xT, w, b, gate, offs, pos1, pos2, 
             round_x(c)
             if c == 1:
                 gates = keep.tile([P, D, V], F32, name="gates", tag="x_raw0")
-                for q in range(D // 2):
-                    nc.scalar.copy(gates[:, 2 * q : 2 * q + 2, :], spreads[q][:])
+                woven = gates[:].rearrange("p d (q i) -> p (d q) i", i=RUN)
+                for e in range(RUN // LINE):
+                    nc.scalar.activation(woven[:, :, e * LINE : (e + 1) * LINE], spreads[e][:].rearrange("p i q -> p q i"), ACT.Copy)
             if c > 0:
                 quantize_x(c - 1)
-                before, now = X_PIECES[c - 1][0], X_PIECES[c][0]
-                if before != now:
+                before = X_PIECES[c - 1][0]
+                if before != X_PIECES[c][0]:
                     gather_words(before)
         quantize_x(len(X_PIECES) - 1)
+        bias_turned = psum.tile([P, P], F32, name="bias_turned", tag="across")
+        nc.tensor.transpose(bias_turned[:], bias_rows[:], ident[:])
+        bias_cols = keep.tile([P, BLOCKS], F32, name="bias_cols", tag="x_bf0", align_bytes=64)
+        nc.scalar.copy(bias_cols[:], bias_turned[:, 0:BLOCKS])
         nc.vector.tensor_copy(got_bytes[:], x_bytes[:].indirect(picked[:]))
 
         for a in range(PASSES):
@@ -234,8 +228,8 @@ def tile_picked_sub_lin_bias_sub_e_kernel(tc, xT, w, b, gate, offs, pos1, pos2, 
             gather_half_words(PASSES - 1, h, after=f"w_raw0_{hi - 1}")
         for a in range(W_PARTS[0]):
             round_w(1, a)
-        first_cols = placed.tile([P, SMALL], F32, name="first_cols", offset=0, align_bytes=64)
-        nc.scalar.copy(first_cols[:], small_cols[:, 0, :])
+        first_cols = placed.tile([P, BLOCKS], F32, name="first_cols", offset=0, align_bytes=64)
+        nc.scalar.copy(first_cols[:], bias_cols[:])
         layer(0)
 
         early_terms = (BLOCKS - 1) * D - 1
@@ -263,7 +257,7 @@ def tile_picked_sub_lin_bias_sub_e_kernel(tc, xT, w, b, gate, offs, pos1, pos2, 
             sum_terms(m)
 
         last = BLOCKS - 1
-        last_terms = keep.tile([P, D + 1, V], F32, name="last_terms", tag="last_cols")
+        last_terms = keep.tile([P, D + 1, V], F32, name="last_terms", tag="x_bf0", align_bytes=64)
         for d in range(D - 1):
             term(last, d, last_terms[:, d, :])
         term(last - 1, D - 1, last_terms[:, D, :])

@@ -24,6 +24,7 @@ BLOCKS = N // P
 V_HALVES = V // P
 S_HALF = S // 2
 FIRST_GROUPS = [(0, S_HALF), (S_HALF, S_HALF // 2), (3 * S_HALF // 2, S_HALF // 2)]
+SHIFT = 32
 LIST_ROWS = 16
 LINE = 4
 RUN = D * V // P
@@ -46,25 +47,25 @@ def tile_picked_sub_lin_bias_sub_e_kernel(tc, xT, w, b, gate, offs, pos1, pos2, 
         neigh = [keep.tile([P, V // LIST_ROWS], U16, name=f"neigh{d}") for d in range(D)]
         gate_runs = keep.tile([P, RUN], F32, name="gate_runs")
         bias_rows = keep.tile([P, P], F32, name="bias_rows")
-        x_raw = [keep.tile([P, PACK, n], F32, name=f"x_raw{c}", tag=f"x_raw{c}") for c, (a, t0, n) in enumerate(X_LOADS)]
-        x_bf = [keep.tile([P, n, PACK], BF16, name=f"x_bf{c}", tag=f"x_bf{c}", align_bytes=64) for c, (a, t0, n, nv) in enumerate(X_PIECES)]
-        x_words = [keep.tile([P, T], U32, name=f"x_words{a}", tag=f"x_words{a}", align_bytes=64) for a in range(PASSES)]
-        x_bytes = keep.tile([P, T], U8, name="x_bytes", align_bytes=64)
+        x_raw = [keep.tile([P, PACK, n], F32, name=f"x_raw{c}", tag=f"x_raw{c}", align_bytes=256) for c, (a, t0, n) in enumerate(X_LOADS)]
+        x_bf = [keep.tile([P, n, PACK], BF16, name=f"x_bf{c}", tag=f"x_bf{c}", align_bytes=256) for c, (a, t0, n, nv) in enumerate(X_PIECES)]
+        x_words = [keep.tile([P, T], U32, name=f"x_words{a}", tag=f"x_words{a}", align_bytes=256) for a in range(PASSES)]
+        x_bytes = keep.tile([P, T], U8, name="x_bytes", align_bytes=256)
         got_words = {}
-        got_bytes = keep.tile([P, S], U8, name="got_bytes", align_bytes=64)
+        got_bytes = keep.tile([P, S], U8, name="got_bytes", align_bytes=256)
         w_raw, w_bf, w_words, w_bytes = {}, {}, {}, {}
         for m in range(BLOCKS):
             for a in range(PASSES):
                 if (m, a) == (1, 1):
-                    w_raw[m, a] = placed.tile([P, PACK, P], F32, name="w_raw1_1", offset=0, align_bytes=64)
+                    w_raw[m, a] = placed.tile([P, PACK, P], F32, name="w_raw1_1", offset=0, align_bytes=256)
                 else:
-                    w_raw[m, a] = keep.tile([P, PACK, P], F32, name=f"w_raw{m}_{a}", tag=f"w_raw{m}_{a}", align_bytes=64)
+                    w_raw[m, a] = keep.tile([P, PACK, P], F32, name=f"w_raw{m}_{a}", tag=f"w_raw{m}_{a}", align_bytes=256)
             for lo, hi in W_PARTS.items():
                 if (m, hi) != (1, PASSES):
-                    w_bf[m, lo] = keep.tile([P, hi - lo, P, PACK], BF16, name=f"w_bf{m}_{lo}", align_bytes=64)
-                w_words[m, lo] = keep.tile([P, hi - lo, P], U32, name=f"w_words{m}_{lo}", align_bytes=64)
-                w_bytes[m, lo] = keep.tile([P, hi - lo, P], U8, name=f"w_bytes{m}_{lo}", align_bytes=64)
-        y = [keep.tile([P, S], F32, name=f"y{m}") for m in range(BLOCKS)]
+                    w_bf[m, lo] = keep.tile([P, hi - lo, P, PACK], BF16, name=f"w_bf{m}_{lo}", align_bytes=256)
+                w_words[m, lo] = keep.tile([P, hi - lo, P], U32, name=f"w_words{m}_{lo}", align_bytes=256)
+                w_bytes[m, lo] = keep.tile([P, hi - lo, P], U8, name=f"w_bytes{m}_{lo}", align_bytes=256)
+        y = [keep.tile([P, S], F32, name=f"y{m}", align_bytes=256) for m in range(BLOCKS)]
         terms = {}
         result = [keep.tile([P, V], F32, name=f"result{m}") for m in range(BLOCKS)]
         ident = keep.tile([P, P], F32, name="ident")
@@ -129,13 +130,13 @@ def tile_picked_sub_lin_bias_sub_e_kernel(tc, xT, w, b, gate, offs, pos1, pos2, 
             )
 
         def gather_words(a):
-            got = keep.tile([P, S], U32, name=f"got_words{a}", align_bytes=64)
+            got = keep.tile([P, S], U32, name=f"got_words{a}", align_bytes=256)
             nc.vector.tensor_copy(got[:], x_words[a][:].indirect(picked[:]))
             for h in range(2):
                 got_words[a, h] = got[:, h * S_HALF : (h + 1) * S_HALF]
 
         def gather_half_words(a, h, after):
-            got = keep.tile([P, S_HALF], U32, name=f"got_words{a}_{h}", tag=after, align_bytes=64)
+            got = keep.tile([P, S_HALF], U32, name=f"got_words{a}_{h}", tag=after, align_bytes=256)
             for first, count in FIRST_GROUPS:
                 if first // S_HALF == h:
                     entries = picked[:, first // LIST_ROWS : (first + count) // LIST_ROWS]
@@ -182,6 +183,9 @@ def tile_picked_sub_lin_bias_sub_e_kernel(tc, xT, w, b, gate, offs, pos1, pos2, 
                 else:
                     nc.scalar.activation(picked_half, accs[h][:], ACT.Identity, bias=bias(m))
 
+        def shifted(tile):
+            return tile[:, SHIFT:].rearrange("p (i v) -> p i v", v=V)
+
         def term(m, d, dst):
             terms[m, d] = dst
             nc.vector.tensor_tensor(dst, y[m][:].indirect(neigh[d][:]), gates[:, d, :], ALU.mult)
@@ -205,7 +209,7 @@ def tile_picked_sub_lin_bias_sub_e_kernel(tc, xT, w, b, gate, offs, pos1, pos2, 
         for c in range(len(X_PIECES)):
             round_x(c)
             if c == 1:
-                gates = keep.tile([P, D, V], F32, name="gates", tag="x_raw0")
+                gates = keep.tile([P, D, V], F32, name="gates", tag="x_raw0", align_bytes=256)
                 woven = gates[:].rearrange("p d (q i) -> p (d q) i", i=RUN)
                 for e in range(RUN // LINE):
                     nc.scalar.activation(woven[:, :, e * LINE : (e + 1) * LINE], spreads[e][:].rearrange("p i q -> p q i"), ACT.Copy)
@@ -217,7 +221,7 @@ def tile_picked_sub_lin_bias_sub_e_kernel(tc, xT, w, b, gate, offs, pos1, pos2, 
         quantize_x(len(X_PIECES) - 1)
         bias_turned = psum.tile([P, P], F32, name="bias_turned", tag="across")
         nc.tensor.transpose(bias_turned[:], bias_rows[:], ident[:])
-        bias_cols = keep.tile([P, BLOCKS], F32, name="bias_cols", tag="x_bf0", align_bytes=64)
+        bias_cols = keep.tile([P, BLOCKS], F32, name="bias_cols", tag="x_bf0", align_bytes=256)
         nc.scalar.copy(bias_cols[:], bias_turned[:, 0:BLOCKS])
         nc.vector.tensor_copy(got_bytes[:], x_bytes[:].indirect(picked[:]))
 
@@ -228,7 +232,7 @@ def tile_picked_sub_lin_bias_sub_e_kernel(tc, xT, w, b, gate, offs, pos1, pos2, 
             gather_half_words(PASSES - 1, h, after=f"w_raw0_{hi - 1}")
         for a in range(W_PARTS[0]):
             round_w(1, a)
-        first_cols = placed.tile([P, BLOCKS], F32, name="first_cols", offset=0, align_bytes=64)
+        first_cols = placed.tile([P, BLOCKS], F32, name="first_cols", offset=0, align_bytes=256)
         nc.scalar.copy(first_cols[:], bias_cols[:])
         layer(0)
 
@@ -239,7 +243,7 @@ def tile_picked_sub_lin_bias_sub_e_kernel(tc, xT, w, b, gate, offs, pos1, pos2, 
             m, lo = calls[first]
             hi = W_PARTS[lo]
             if (m, hi) == (1, PASSES):
-                w_bf[m, lo] = placed.tile([P, hi - lo, P, PACK], BF16, name=f"w_bf{m}_{lo}", offset=0, align_bytes=64)
+                w_bf[m, lo] = placed.tile([P, hi - lo, P, PACK], BF16, name=f"w_bf{m}_{lo}", offset=0, align_bytes=256)
             for a in range(lo, hi):
                 if first > 0:
                     round_w(m, a)
@@ -247,9 +251,9 @@ def tile_picked_sub_lin_bias_sub_e_kernel(tc, xT, w, b, gate, offs, pos1, pos2, 
             if hi == PASSES:
                 layer(m)
             if first == 0:
-                run = placed.tile([P, end - first, V], F32, name="run0", offset=4 * V, align_bytes=64)
+                run = shifted(placed.tile([P, (end - first) * V + SHIFT], F32, name="run0", offset=4 * V, align_bytes=256))
             else:
-                run = keep.tile([P, end - first + (BLOCKS - 2 if end == early_terms else 0), V], F32, name=f"run{first}", tag=f"w_raw{m}_{hi - 1}", align_bytes=64)
+                run = shifted(keep.tile([P, (end - first + (BLOCKS - 2 if end == early_terms else 0)) * V + SHIFT], F32, name=f"run{first}", tag=f"w_raw{m}_{hi - 1}", align_bytes=256))
             spare = run[:, end - first :, :]
             for i in range(first, end):
                 term(i // D, i % D, run[:, i - first, :])
@@ -257,7 +261,7 @@ def tile_picked_sub_lin_bias_sub_e_kernel(tc, xT, w, b, gate, offs, pos1, pos2, 
             sum_terms(m)
 
         last = BLOCKS - 1
-        last_terms = keep.tile([P, D + 1, V], F32, name="last_terms", tag="x_bf0", align_bytes=64)
+        last_terms = shifted(keep.tile([P, (D + 1) * V + SHIFT], F32, name="last_terms", tag="x_bf0", align_bytes=256))
         for d in range(D - 1):
             term(last, d, last_terms[:, d, :])
         term(last - 1, D - 1, last_terms[:, D, :])

@@ -23,17 +23,16 @@ PASSES = K // K_PASS
 BLOCKS = N // P
 V_HALVES = V // P
 S_HALF = S // 2
-FIRST_GROUPS = [(0, S_HALF), (S_HALF, S_HALF // 2), (3 * S_HALF // 2, S_HALF // 2)]
 SHIFT = 32
 LIST_ROWS = 16
 LINE = 4
 RUN = D * V // P
-
-X_LOADS = [(0, 0, T), (1, 0, T), (2, 0, 512), (2, 512, 256), (2, 768, 256)]
-X_PIECES = [(0, 0, 512, 512), (0, 512, 512, 64), (1, 0, 512, 512), (1, 512, 512, 64),
-            (2, 0, 512, 128), (2, 512, 256, 0), (2, 768, 256, 160)]
-W_PARTS = {0: 2, 2: 3}
-TERMS_AHEAD = {(1, 0): 0, (1, 2): 2, (2, 0): 4, (2, 2): 5, (3, 0): 7, (3, 2): 8}
+KIB = 1024
+HEAD_SHARE = 304
+SLOT = 6 * KIB
+X_LOADS = [(a, j, 1) for a in range(PASSES) for j in range(PACK)]
+VECTOR_ENTRIES = {(0, 1): S, (0, 3): S, (1, 1): S, (2, 1): 128, (2, 2): 320, (2, 3): 256}
+CALLS = {(0, 1): 2, (0, 2): 3, (1, 1): 3, (2, 1): 3, (3, 1): 3}
 
 
 def tile_picked_sub_lin_bias_sub_e_kernel(tc, xT, w, b, gate, offs, pos1, pos2, pos3, pos4, out):
@@ -47,110 +46,113 @@ def tile_picked_sub_lin_bias_sub_e_kernel(tc, xT, w, b, gate, offs, pos1, pos2, 
         neigh = [keep.tile([P, V // LIST_ROWS], U16, name=f"neigh{d}") for d in range(D)]
         gate_runs = keep.tile([P, RUN], F32, name="gate_runs")
         bias_rows = keep.tile([P, P], F32, name="bias_rows")
-        x_raw = [keep.tile([P, PACK, n], F32, name=f"x_raw{c}", tag=f"x_raw{c}", align_bytes=256) for c, (a, t0, n) in enumerate(X_LOADS)]
-        x_bf = [keep.tile([P, n, PACK], BF16, name=f"x_bf{c}", tag=f"x_bf{c}", align_bytes=256) for c, (a, t0, n, nv) in enumerate(X_PIECES)]
-        x_words = [keep.tile([P, T], U32, name=f"x_words{a}", tag=f"x_words{a}", align_bytes=256) for a in range(PASSES)]
-        x_bytes = keep.tile([P, T], U8, name="x_bytes", align_bytes=256)
-        got_words = {}
-        got_bytes = keep.tile([P, S], U8, name="got_bytes", align_bytes=256)
-        w_raw, w_bf, w_words, w_bytes = {}, {}, {}, {}
-        for m in range(BLOCKS):
-            for a in range(PASSES):
-                if (m, a) == (1, 1):
-                    w_raw[m, a] = placed.tile([P, PACK, P], F32, name="w_raw1_1", offset=0, align_bytes=256)
-                else:
-                    w_raw[m, a] = keep.tile([P, PACK, P], F32, name=f"w_raw{m}_{a}", tag=f"w_raw{m}_{a}", align_bytes=256)
-            for lo, hi in W_PARTS.items():
-                if (m, hi) != (1, PASSES):
-                    w_bf[m, lo] = keep.tile([P, hi - lo, P, PACK], BF16, name=f"w_bf{m}_{lo}", align_bytes=256)
-                w_words[m, lo] = keep.tile([P, hi - lo, P], U32, name=f"w_words{m}_{lo}", align_bytes=256)
-                w_bytes[m, lo] = keep.tile([P, hi - lo, P], U8, name=f"w_bytes{m}_{lo}", align_bytes=256)
-        y = [keep.tile([P, S], F32, name=f"y{m}", align_bytes=256) for m in range(BLOCKS)]
+        planes = [(a, j) for a in range(PASSES) for j in range(PACK)]
+        parts = [(m, a) for m in range(BLOCKS) for a in range(1, PASSES)]
+        slot = {part: i * SLOT for i, part in enumerate(parts)}
+        last_plane = (len(parts) + 1) * SLOT
+        x_loads = {load: keep.tile([P, load[2], T], F32, name=f"x_raw{load[0]}_{load[1]}", align_bytes=256) for load in X_LOADS[:-1]}
+        x_loads[X_LOADS[-1]] = placed.tile([P, 1, T], F32, name="x_raw_last", offset=last_plane, align_bytes=256)
+        x_raw = {(a, j + i): tile[:, i, :] for (a, j, count), tile in x_loads.items() for i in range(count)}
+        got = [keep.tile([P, PACK, S], F32, name=f"got{a}", align_bytes=256) for a in range(PASSES)]
+        x_bf = [keep.tile([P, S, PACK], BF16, name=f"x_bf{a}", align_bytes=256) for a in range(PASSES)]
+        x_words = [keep.tile([P, S], U32, name=f"x_words{a}", align_bytes=256) for a in range(PASSES)]
+        x_bytes = [keep.tile([P, S], U8, name=f"x_bytes{a}", align_bytes=256) for a in range(PASSES)]
+        slot[1, 1] = slot[1, 2] - 2 * KIB
+        w_raw = {(m, a): placed.tile([P, PACK, P], F32, name=f"w_raw{m}_{a}", offset=slot[m, a], align_bytes=256)[:] for m, a in parts}
+        w_words = {(m, lo): keep.tile([P, hi - lo, P], U32, name=f"w_words{m}_{lo}", align_bytes=256) for (m, lo), hi in CALLS.items()}
+        w_bytes = {(m, lo): keep.tile([P, hi - lo, P], U8, name=f"w_bytes{m}_{lo}", align_bytes=256) for (m, lo), hi in CALLS.items()}
+        w_bf = {}
+        head_raw = keep.tile([P, PACK, N], F32, name="head_raw", align_bytes=256)
+        head_bf = keep.tile([P, N, PACK], BF16, name="head_bf", align_bytes=256)
+        head_words = keep.tile([P, N], U32, name="head_words", align_bytes=256)
+        head_bytes = keep.tile([P, N], U8, name="head_bytes", align_bytes=256)
+        y = {}
         terms = {}
-        result = [keep.tile([P, V], F32, name=f"result{m}") for m in range(BLOCKS)]
+        result = {m: keep.tile([P, V], F32, name=f"result{m}")[:] for m in range(BLOCKS)}
         ident = keep.tile([P, P], F32, name="ident")
+        gates = keep.tile([P, D, V], F32, name="gates", align_bytes=256)
+        bias_cols = [keep.tile([P, 1], F32, name=f"bias{m}", tag=f"bias{m}", align_bytes=256)[:] for m in range(BLOCKS)]
 
-        def load_x(c):
-            a, t0, n = X_LOADS[c]
-            rows = xT[a * K_PASS : (a + 1) * K_PASS, t0 : t0 + n]
-            nc.sync.dma_start(out=x_raw[c][:], in_=rows.rearrange("(p j) t -> p j t", j=PACK))
+        def load_x(a, j, count):
+            rows = xT[a * K_PASS : (a + 1) * K_PASS, :].rearrange("(p j) t -> p j t", j=PACK)
+            nc.sync.dma_start(out=x_loads[a, j, count][:], in_=rows[:, j : j + count, :])
 
         def load_w(m, a):
             rows = w[a * K_PASS : (a + 1) * K_PASS, m * P : (m + 1) * P]
-            nc.sync.dma_start(out=w_raw[m, a][:], in_=rows.rearrange("(p j) n -> p j n", j=PACK))
+            nc.sync.dma_start(out=w_raw[m, a], in_=rows.rearrange("(p j) n -> p j n", j=PACK))
 
         nc.vector.memset(bias_rows[:], 0.0)
-        load_x(0)
+        load_x(*X_LOADS[0])
+        nc.sync.dma_start(picked[:], offs)
         nc.sync.dma_start(out=gate_runs[:], in_=gate[:, 0, :].rearrange("d (q i) -> d q i", i=RUN))
         nc.sync.dma_start(out=bias_rows[0:BLOCKS, :], in_=b.rearrange("(m q) o -> m (q o)", q=P))
-        nc.sync.dma_start(picked[:], offs)
-        for c in range(1, len(X_LOADS)):
-            load_x(c)
-        for m in range(BLOCKS):
-            for a in range(PASSES):
-                load_w(m, a)
-                if (m, a) == (1, 1):
-                    for d, places in enumerate((pos1, pos2, pos3, pos4)):
-                        nc.sync.dma_start(neigh[d][:], places)
+        for a, j, count in X_LOADS[1:]:
+            if (a, j) == (PASSES - 1, 1):
+                nc.sync.dma_start(out=head_raw[:], in_=w[0:K_PASS, :].rearrange("(p j) n -> p j n", j=PACK))
+            load_x(a, j, count)
+        for m, a in parts:
+            load_w(m, a)
+            if a == PASSES - 1 and m in (1, 2):
+                for d in (2 * m - 2, 2 * m - 1):
+                    nc.sync.dma_start(neigh[d][:], (pos1, pos2, pos3, pos4)[d])
 
-        nc.vector.memset(x_bytes[:].bitcast(U32), 0)
         make_identity(nc, ident[:])
 
         v_halves = [slice(h * P, (h + 1) * P) for h in range(V_HALVES)]
-        spreads = []
+        woven = gates[:].rearrange("p d (q i) -> p (d q) i", i=RUN)
         for e in range(RUN // LINE):
-            spreads.append(psum.tile([P, LINE, P], F32, name=f"spread{e}", tag=f"back{e}"))
+            spread = psum.tile([P, LINE, P], F32, name=f"spread{e}", tag=f"back{e}")
             for i in range(LINE):
                 column = gate_runs[:, e * LINE + i : e * LINE + i + 1]
-                nc.tensor.transpose(spreads[e][:, i, :], column.to_broadcast([P, P]), ident[:])
+                nc.tensor.transpose(spread[:, i, :], column.to_broadcast([P, P]), ident[:])
+            nc.vector.tensor_copy(woven[:, :, e * LINE : (e + 1) * LINE], spread[:].rearrange("p i q -> p q i"))
+        bias_turned = psum.tile([P, P], F32, name="bias_turned", tag="across")
+        nc.tensor.transpose(bias_turned[:], bias_rows[:], ident[:])
+        for m in range(BLOCKS):
+            nc.vector.tensor_copy(bias_cols[m], bias_turned[:, m : m + 1])
 
-        def bias(m):
-            return bias_cols[:, m : m + 1]
+        def gather(a, j, first, count, on_vector):
+            window = x_raw[a, j].indirect(picked[:, first // LIST_ROWS : (first + count) // LIST_ROWS])
+            if on_vector:
+                nc.vector.tensor_copy(got[a][:, j, first : first + count], window)
+            else:
+                nc.scalar.activation(got[a][:, j, first : first + count], window, ACT.Copy)
 
-        def round_x(c):
-            a, t0, n, nv = X_PIECES[c]
-            load = max(i for i, (b0, s0, n0) in enumerate(X_LOADS) if (b0, s0) <= (a, t0))
-            skip = t0 - X_LOADS[load][1]
-            for lo, hi in ((nv, n), (0, nv)):
-                if lo == hi:
-                    continue
-                src = x_raw[load][:, :, skip + lo : skip + hi].rearrange("p j (c i) -> p c j i", i=LINE)
-                dst = x_bf[c][:, lo:hi, :].rearrange("p (c i) j -> p c j i", i=LINE)
-                if hi == nv and lo == 0:
-                    nc.vector.tensor_copy(dst, src)
-                else:
-                    nc.scalar.activation(dst, src, ACT.Copy)
+        def weave(dst, src, on_vector):
+            src = src.rearrange("p j (c i) -> p c j i", i=LINE)
+            dst = dst.rearrange("p (c i) j -> p c j i", i=LINE)
+            if on_vector:
+                nc.vector.tensor_copy(dst, src)
+            else:
+                nc.scalar.activation(dst, src, ACT.Copy)
 
-        def quantize_x(c):
-            a, t0, n, nv = X_PIECES[c]
+        def weave_x(a, first, end, on_vector):
+            weave(x_bf[a][:, first:end, :], got[a][:, :, first:end], on_vector)
+
+        def quantize_x(a, first, end):
             nc.vector.quantize_mx(
-                out=x_words[a][:, t0 : t0 + n].bitcast(FP8X4),
-                scales=x_bytes[PACK * a :, t0 : t0 + n],
-                in_=x_bf[c][:].rearrange("p t j -> p (t j)"),
+                out=x_words[a][:, first:end].bitcast(FP8X4),
+                scales=x_bytes[a][:, first:end],
+                in_=x_bf[a][:, first:end, :].rearrange("p t j -> p (t j)"),
             )
 
-        def gather_words(a):
-            got = keep.tile([P, S], U32, name=f"got_words{a}", align_bytes=256)
-            nc.vector.tensor_copy(got[:], x_words[a][:].indirect(picked[:]))
-            for h in range(2):
-                got_words[a, h] = got[:, h * S_HALF : (h + 1) * S_HALF]
+        def weights(m, a):
+            if a == 0:
+                return head_words[:, m * P : (m + 1) * P], head_bytes[:, m * P : (m + 1) * P]
+            lo = max(lo for block, lo in CALLS if block == m and lo <= a)
+            return w_words[m, lo][:, a - lo, :], w_bytes[m, lo][:, a - lo, :]
 
-        def gather_half_words(a, h, after):
-            got = keep.tile([P, S_HALF], U32, name=f"got_words{a}_{h}", tag=after, align_bytes=256)
-            for first, count in FIRST_GROUPS:
-                if first // S_HALF == h:
-                    entries = picked[:, first // LIST_ROWS : (first + count) // LIST_ROWS]
-                    nc.vector.tensor_copy(got[:, first % S_HALF : first % S_HALF + count], x_words[a][:].indirect(entries))
-            got_words[a, h] = got[:]
-
-        def part_of(a):
-            return max(lo for lo in W_PARTS if lo <= a)
-
-        def round_w(m, a):
-            lo = part_of(a)
-            src = w_raw[m, a][:].rearrange("p j (c i) -> p c j i", i=LINE)
-            dst = w_bf[m, lo][:, a - lo, :, :].rearrange("p (c i) j -> p c j i", i=LINE)
-            nc.scalar.activation(dst, src, ACT.Copy)
+        def round_w(m, lo, on_vector=(), passes=None):
+            hi = CALLS[m, lo]
+            shape, name = [P, hi - lo, P, PACK], f"w_bf{m}_{lo}"
+            if (m, lo) in w_bf:
+                pass
+            elif m < 2:
+                w_bf[m, lo] = placed.tile(shape, BF16, name=name, offset=last_plane + (2 * m + lo - 1) * KIB, align_bytes=256)
+            else:
+                w_bf[m, lo] = keep.tile(shape, BF16, name=name, tag=f"bias{m - 2}", align_bytes=256)
+            for a in passes or range(lo, hi):
+                weave(w_bf[m, lo][:, a - lo, :, :], w_raw[m, a], a in on_vector)
 
         def quantize_w(m, lo):
             nc.vector.quantize_mx(
@@ -160,28 +162,28 @@ def tile_picked_sub_lin_bias_sub_e_kernel(tc, xT, w, b, gate, offs, pos1, pos2, 
             )
 
         def layer(m):
-            groups = FIRST_GROUPS if m == 0 else [(0, S_HALF), (S_HALF, S_HALF)]
-            accs = [psum.tile([P, n], F32, name=f"acc{m}_{h}", tag=f"acc{m % 2}_{h}") for h, (first, n) in enumerate(groups)]
-            for a in range(PASSES):
-                lo = part_of(a)
-                for h, (first, n) in enumerate(groups):
-                    nc.tensor.matmul_mx(
-                        out=accs[h][:],
-                        lhsT=w_words[m, lo][:, a - lo, :].bitcast(FP8X4),
-                        lhsT_scale=w_bytes[m, lo][:, a - lo, :],
-                        rhs=got_words[a, first // S_HALF][:, first % S_HALF : first % S_HALF + n].bitcast(FP8X4),
-                        rhs_scale=got_bytes[PACK * a :, first : first + n],
-                        start=(a == 0),
-                        stop=(a == PASSES - 1),
-                    )
-            for h, (first, n) in enumerate(groups):
-                picked_half = y[m][:, first : first + n]
-                if (m, h) == (0, 0):
-                    nc.vector.tensor_scalar_add(picked_half, accs[h][:], bias(m))
-                elif m == 0:
-                    nc.scalar.activation(picked_half, accs[h][:], ACT.Identity, bias=first_cols[:, 0:1])
-                else:
-                    nc.scalar.activation(picked_half, accs[h][:], ACT.Identity, bias=bias(m))
+            groups = [slice(0, S)] if m in (1, 2) else [slice(0, S_HALF), slice(S_HALF, S)]
+            accs = [psum.tile([P, cols.stop - cols.start], F32, name=f"acc{m}_{h}", tag=f"acc{m % 3}_{h}") for h, cols in enumerate(groups)]
+            steps = [(a, h) for a in range(PASSES) for h in range(len(groups))]
+            for a, h in steps if m == 0 else sorted(steps, key=lambda step: step[1]):
+                words, scales = weights(m, a)
+                nc.tensor.matmul_mx(
+                    out=accs[h][:],
+                    lhsT=words.bitcast(FP8X4),
+                    lhsT_scale=scales,
+                    rhs=x_words[a][:, groups[h]].bitcast(FP8X4),
+                    rhs_scale=x_bytes[a][:, groups[h]],
+                    start=(a == 0),
+                    stop=(a == PASSES - 1),
+                )
+            if m == 2:
+                y[m] = placed.tile([P, S], F32, name=f"y{m}", offset=slot[3, 1], align_bytes=256)
+            elif m + 1 < BLOCKS:
+                y[m] = placed.tile([P, S], F32, name=f"y{m}", offset=slot[m + 1, PASSES - 1] - KIB, align_bytes=256)
+            else:
+                y[m] = keep.tile([P, S], F32, name=f"y{m}", align_bytes=256)
+            for h, cols in enumerate(groups):
+                nc.scalar.activation(y[m][:, cols], accs[h][:], ACT.Identity, bias=bias_cols[m])
 
         def shifted(tile):
             return tile[:, SHIFT:].rearrange("p (i v) -> p i v", v=V)
@@ -191,94 +193,113 @@ def tile_picked_sub_lin_bias_sub_e_kernel(tc, xT, w, b, gate, offs, pos1, pos2, 
             nc.vector.tensor_tensor(dst, y[m][:].indirect(neigh[d][:]), gates[:, d, :], ALU.mult)
 
         def store(m):
-            nc.sync.dma_start(out=out[m * P : (m + 1) * P, :], in_=result[m][:])
+            nc.sync.dma_start(out=out[m * P : (m + 1) * P, :], in_=result[m])
 
-        def sum_terms(m):
-            across = psum.tile([P, V], F32, name=f"across{m}", tag="across" if m == 0 else f"acc{m % 2}_0")
-            for cols in v_halves:
-                for d in range(D):
-                    nc.tensor.matmul(across[:, cols], terms[m, d][:, cols], ident[:], start=(d == 0), stop=(d == D - 1), is_transpose=True)
-            turned = spare[:, m, :]
-            nc.scalar.copy(turned, across[:])
-            back = psum.tile([P, V], F32, name=f"back{m}", tag=f"back{m % 2}")
-            for cols in v_halves:
-                nc.tensor.transpose(back[:, cols], turned[:, cols], ident[:])
-            nc.scalar.copy(result[m][:], back[:])
-            store(m)
-
-        for c in range(len(X_PIECES)):
-            round_x(c)
-            if c == 1:
-                gates = keep.tile([P, D, V], F32, name="gates", tag="x_raw0", align_bytes=256)
-                woven = gates[:].rearrange("p d (q i) -> p (d q) i", i=RUN)
-                for e in range(RUN // LINE):
-                    nc.scalar.activation(woven[:, :, e * LINE : (e + 1) * LINE], spreads[e][:].rearrange("p i q -> p q i"), ACT.Copy)
-            if c > 0:
-                quantize_x(c - 1)
-                before = X_PIECES[c - 1][0]
-                if before != X_PIECES[c][0]:
-                    gather_words(before)
-        quantize_x(len(X_PIECES) - 1)
-        bias_turned = psum.tile([P, P], F32, name="bias_turned", tag="across")
-        nc.tensor.transpose(bias_turned[:], bias_rows[:], ident[:])
-        bias_cols = keep.tile([P, BLOCKS], F32, name="bias_cols", tag="x_bf0", align_bytes=256)
-        nc.scalar.copy(bias_cols[:], bias_turned[:, 0:BLOCKS])
-        nc.vector.tensor_copy(got_bytes[:], x_bytes[:].indirect(picked[:]))
-
-        for a in range(PASSES):
-            round_w(0, a)
-        for h, (lo, hi) in enumerate(W_PARTS.items()):
-            quantize_w(0, lo)
-            gather_half_words(PASSES - 1, h, after=f"w_raw0_{hi - 1}")
-        for a in range(W_PARTS[0]):
-            round_w(1, a)
-        first_cols = placed.tile([P, BLOCKS], F32, name="first_cols", offset=0, align_bytes=256)
-        nc.scalar.copy(first_cols[:], bias_cols[:])
+        last_pass = PASSES - 1
+        for a, j in planes:
+            share = VECTOR_ENTRIES.get((a, j), 0)
+            if share:
+                gather(a, j, 0, share, True)
+            if share < S:
+                gather(a, j, share, S - share, False)
+            if j == PACK - 1 and a < last_pass:
+                weave_x(a, 0, S, True)
+                quantize_x(a, 0, S)
+            if (a, j) == (last_pass, 0):
+                weave(head_bf[:, HEAD_SHARE:, :], head_raw[:, :, HEAD_SHARE:], False)
+                weave(head_bf[:, :HEAD_SHARE, :], head_raw[:, :, :HEAD_SHARE], True)
+                nc.vector.quantize_mx(out=head_words[:].bitcast(FP8X4), scales=head_bytes[:], in_=head_bf[:].rearrange("p n j -> p (n j)"))
+        for h in range(2):
+            weave_x(last_pass, h * S_HALF, (h + 1) * S_HALF, h == 0)
+        round_w(0, 1, (1,))
+        quantize_x(last_pass, 0, S_HALF)
+        quantize_w(0, 1)
+        quantize_x(last_pass, S_HALF, S)
+        round_w(0, 2)
+        quantize_w(0, 2)
+        round_w(1, 1, (2,))
         layer(0)
+        quantize_w(1, 1)
 
-        early_terms = (BLOCKS - 1) * D - 1
-        calls = {ahead: call for call, ahead in TERMS_AHEAD.items()}
-        starts = sorted(calls) + [early_terms]
-        for first, end in zip(starts, starts[1:]):
-            m, lo = calls[first]
-            hi = W_PARTS[lo]
-            if (m, hi) == (1, PASSES):
-                w_bf[m, lo] = placed.tile([P, hi - lo, P, PACK], BF16, name=f"w_bf{m}_{lo}", offset=0, align_bytes=256)
-            for a in range(lo, hi):
-                if first > 0:
-                    round_w(m, a)
-            quantize_w(m, lo)
-            if hi == PASSES:
-                layer(m)
-            if first == 0:
-                run = shifted(placed.tile([P, (end - first) * V + SHIFT], F32, name="run0", offset=4 * V, align_bytes=256))
-            else:
-                run = shifted(keep.tile([P, (end - first + (BLOCKS - 2 if end == early_terms else 0)) * V + SHIFT], F32, name=f"run{first}", tag=f"w_raw{m}_{hi - 1}", align_bytes=256))
-            spare = run[:, end - first :, :]
-            for i in range(first, end):
-                term(i // D, i % D, run[:, i - first, :])
-        for m in range(BLOCKS - 2):
-            sum_terms(m)
+        def term_tile(count, name, offset=None):
+            if offset is None:
+                return shifted(keep.tile([P, count * V + SHIFT], F32, name=name, align_bytes=256))
+            return shifted(placed.tile([P, count * V + SHIFT], F32, name=name, offset=offset, align_bytes=256))
 
-        last = BLOCKS - 1
-        last_terms = shifted(keep.tile([P, (D + 1) * V + SHIFT], F32, name="last_terms", tag="x_bf0", align_bytes=256))
-        for d in range(D - 1):
-            term(last, d, last_terms[:, d, :])
-        term(last - 1, D - 1, last_terms[:, D, :])
-        term(last, D - 1, last_terms[:, D - 1, :])
-        whole = psum.tile([P, V], F32, name="across_whole", tag="across")
-        banks = {last - 1: [whole[:, cols] for cols in v_halves],
-                 last: [psum.tile([P, P], F32, name=f"across_half{h}", tag=f"acc0_{h}")[:] for h in range(V_HALVES)]}
-        steps = {last - 1: [(h, d) for h in range(V_HALVES) for d in range(D - 1)],
-                 last: [(h, d) for d in range(D - 1) for h in range(V_HALVES)]}
-        for m in (last - 1, last):
-            for h, d in steps[m]:
-                nc.tensor.matmul(banks[m][h], terms[m, d][:, v_halves[h]], ident[:], start=(d == 0), stop=(d == D - 2), is_transpose=True)
-            turned = keep.tile([P, V], F32, name=f"turned{m}")
-            back = psum.tile([P, V], F32, name=f"back{m}", tag=f"back{m % 2}")
+        def across_halves(m, order, tags, held):
+            banks = [psum.tile([P, P], F32, name=f"across{m}_{h}", tag=tag) for h, tag in enumerate(tags)]
+            for i, d in enumerate(order):
+                for h, cols in enumerate(v_halves):
+                    nc.tensor.matmul(banks[h][:], terms[m, d][:, cols], ident[:], start=(i == 0), stop=(i == len(order) - 1), is_transpose=True)
+            turned[m] = held
             for h, cols in enumerate(v_halves):
-                nc.scalar.copy(turned[:, cols], banks[m][h])
+                nc.scalar.copy(held[:, cols], banks[h][:])
+
+        def back(m, tag):
+            bank = psum.tile([P, V], F32, name=f"back{m}", tag=tag)
             for cols in v_halves:
-                nc.tensor.transpose(back[:, cols], turned[:, cols], ident[:])
-            nc.vector.tensor_tensor(result[m][:], back[:], terms[m, D - 1], ALU.add)
+                nc.tensor.transpose(bank[:, cols], turned[m][:, cols], ident[:])
+            return bank
+
+        def fetch(m, d, dst):
+            fetched[m, d] = dst
+            nc.scalar.activation(dst, y[m][:].indirect(neigh[d][:]), ACT.Copy)
+
+        def weigh(m, d, dst):
+            terms[m, d] = dst
+            nc.vector.tensor_tensor(dst, fetched[m, d], gates[:, d, :], ALU.mult)
+
+        turned = {}
+        free_terms = term_tile(2, "free_terms")
+        round_w(2, 1)
+        layer(1)
+        for d in range(2):
+            term(0, d, free_terms[:, d, :])
+        quantize_w(2, 1)
+        held_terms = term_tile(4, "held_terms", slot[2, 2] + KIB)
+        for d in (2, 3):
+            term(0, d, held_terms[:, d - 2, :])
+        round_w(3, 1, (), (1,))
+        layer(2)
+        round_w(3, 1, (), (2,))
+        for d in range(2):
+            term(1, d, held_terms[:, 2 + d, :])
+        quantize_w(3, 1)
+        held_terms = term_tile(1, "later_terms", slot[3, 2] + KIB)
+        term(1, 2, held_terms[:, 0, :])
+        fetched = {}
+        first_fetched = placed.tile([P, 2, V], F32, name="first_fetched", offset=slot[3, 2] - KIB, align_bytes=256)
+        for d in range(2):
+            fetch(2, d, first_fetched[:, d, :])
+        layer(3)
+        spare = shifted(keep.tile([P, (BLOCKS + 1) * V + SHIFT], F32, name="spare", tag="bias3", align_bytes=256))
+        fetch(3, 0, spare[:, BLOCKS, :])
+        last_terms = term_tile(2 * D - 1, "last_terms")
+        weigh(2, 0, last_terms[:, D, :])
+        term(2, 2, last_terms[:, D + 2, :])
+        weigh(2, 1, last_terms[:, D + 1, :])
+        for d in (1, 2):
+            term(3, d, last_terms[:, d, :])
+        weigh(3, 0, last_terms[:, 0, :])
+        term(1, 3, gates[:, 1, :])
+        term(2, 3, gates[:, 2, :])
+        term(3, 3, last_terms[:, 3, :])
+
+        early = psum.tile([P, 2, V], F32, name="early_across", tag="back1")
+        for m in range(2):
+            for cols in v_halves:
+                for d in range(D - m):
+                    nc.tensor.matmul(early[:, m, cols], terms[m, d][:, cols], ident[:], start=(d == 0), stop=(d == D - m - 1), is_transpose=True)
+        nc.scalar.copy(spare[:, 0:2, :], early[:])
+        across_halves(2, (0, 2, 1), ("acc2_0", "across"), spare[:, 2, :])
+        early_back = psum.tile([P, 2, V], F32, name="early_back", tag="back0")
+        for m in range(2):
+            for cols in v_halves:
+                nc.tensor.transpose(early_back[:, m, cols], spare[:, m, cols], ident[:])
+        nc.scalar.copy(result[0], early_back[:, 0, :])
+        store(0)
+        across_halves(3, (1, 2, 0), ("acc0_0", "acc0_1"), spare[:, 3, :])
+        banks = {1: early_back[:, 1, :], 2: back(2, "acc1_0")[:], 3: back(3, "eighth")[:]}
+        for m in (1, 2, 3):
+            nc.vector.tensor_tensor(result[m], banks[m], terms[m, D - 1], ALU.add)
             store(m)

from contextlib import ExitStack

import concourse.mybir as mybir
from concourse.masks import make_identity

K, T, D, S, V, N = 1536, 1024, 4, 512, 256, 512
FLOPS = 2 * K * N * S
BYTES = 4 * (K * T + K * N + N + D * V + N * V) + 2 * 128 * (S + D * V) // 16

F32 = mybir.dt.float32
BF16 = mybir.dt.bfloat16
U32 = mybir.dt.uint32
U16 = mybir.dt.uint16
U8 = mybir.dt.uint8
FP8X4 = mybir.dt.float8_e4m3fn_x4
ACT = mybir.ActivationFunctionType
ALU = mybir.AluOpType

P = 128
PACK = 4
K_PASS = P * PACK
PASSES = K // K_PASS
BLOCKS = N // P
V_HALVES = V // P
S_HALF = S // 2
SHIFT = 32
LIST_ROWS = 16
LINE = 4
RUN = D * V // P
KIB = 1024
HEAD_SHARE = 304
SLOT = 6 * KIB
X_LOADS = [(a, j, 1) for a in range(PASSES) for j in range(PACK)]
VECTOR_ENTRIES = {(0, 1): S, (0, 3): S, (1, 1): S, (2, 1): 128, (2, 2): 320, (2, 3): 256}
CALLS = {(0, 1): 2, (0, 2): 3, (1, 1): 3, (2, 1): 3, (3, 1): 3}


def tile_picked_sub_lin_bias_sub_e_kernel(tc, xT, w, b, gate, offs, pos1, pos2, pos3, pos4, out):
    nc = tc.nc
    with ExitStack() as ctx:
        keep = ctx.enter_context(tc.tile_pool(name="keep", bufs=1))
        placed = ctx.enter_context(tc.tile_pool(name="placed", bufs=1))
        psum = ctx.enter_context(tc.psum_pool(name="psum", bufs=1))

        picked = keep.tile([P, S // LIST_ROWS], U16, name="picked")
        neigh = [keep.tile([P, V // LIST_ROWS], U16, name=f"neigh{d}") for d in range(D)]
        gate_runs = keep.tile([P, RUN], F32, name="gate_runs")
        bias_rows = keep.tile([P, P], F32, name="bias_rows")
        planes = [(a, j) for a in range(PASSES) for j in range(PACK)]
        parts = [(m, a) for m in range(BLOCKS) for a in range(1, PASSES)]
        slot = {part: i * SLOT for i, part in enumerate(parts)}
        last_plane = (len(parts) + 1) * SLOT
        x_loads = {load: keep.tile([P, load[2], T], F32, name=f"x_raw{load[0]}_{load[1]}", align_bytes=256) for load in X_LOADS[:-1]}
        x_loads[X_LOADS[-1]] = placed.tile([P, 1, T], F32, name="x_raw_last", offset=last_plane, align_bytes=256)
        x_raw = {(a, j + i): tile[:, i, :] for (a, j, count), tile in x_loads.items() for i in range(count)}
        got = [keep.tile([P, PACK, S], F32, name=f"got{a}", align_bytes=256) for a in range(PASSES)]
        x_bf = [keep.tile([P, S, PACK], BF16, name=f"x_bf{a}", align_bytes=256) for a in range(PASSES)]
        x_words = [keep.tile([P, S], U32, name=f"x_words{a}", align_bytes=256) for a in range(PASSES)]
        x_bytes = [keep.tile([P, S], U8, name=f"x_bytes{a}", align_bytes=256) for a in range(PASSES)]
        slot[1, 1] = slot[1, 2] - 2 * KIB
        w_raw = {(m, a): placed.tile([P, PACK, P], F32, name=f"w_raw{m}_{a}", offset=slot[m, a], align_bytes=256)[:] for m, a in parts}
        w_words = {(m, lo): keep.tile([P, hi - lo, P], U32, name=f"w_words{m}_{lo}", align_bytes=256) for (m, lo), hi in CALLS.items()}
        w_bytes = {(m, lo): keep.tile([P, hi - lo, P], U8, name=f"w_bytes{m}_{lo}", align_bytes=256) for (m, lo), hi in CALLS.items()}
        w_bf = {}
        head_raw = keep.tile([P, PACK, N], F32, name="head_raw", align_bytes=256)
        head_bf = keep.tile([P, N, PACK], BF16, name="head_bf", align_bytes=256)
        head_words = keep.tile([P, N], U32, name="head_words", align_bytes=256)
        head_bytes = keep.tile([P, N], U8, name="head_bytes", align_bytes=256)
        y = {}
        terms = {}
        result = {m: keep.tile([P, V], F32, name=f"result{m}")[:] for m in range(BLOCKS)}
        ident = keep.tile([P, P], F32, name="ident")
        gates = keep.tile([P, D, V], F32, name="gates", align_bytes=256)
        bias_cols = [keep.tile([P, 1], F32, name=f"bias{m}", tag=f"bias{m}", align_bytes=256)[:] for m in range(BLOCKS)]

        def load_x(a, j, count):
            rows = xT[a * K_PASS : (a + 1) * K_PASS, :].rearrange("(p j) t -> p j t", j=PACK)
            nc.sync.dma_start(out=x_loads[a, j, count][:], in_=rows[:, j : j + count, :])

        def load_w(m, a):
            rows = w[a * K_PASS : (a + 1) * K_PASS, m * P : (m + 1) * P]
            nc.sync.dma_start(out=w_raw[m, a], in_=rows.rearrange("(p j) n -> p j n", j=PACK))

        nc.vector.memset(bias_rows[:], 0.0)
        load_x(*X_LOADS[0])
        nc.sync.dma_start(picked[:], offs)
        nc.sync.dma_start(out=gate_runs[:], in_=gate[:, 0, :].rearrange("d (q i) -> d q i", i=RUN))
        nc.sync.dma_start(out=bias_rows[0:BLOCKS, :], in_=b.rearrange("(m q) o -> m (q o)", q=P))
        for a, j, count in X_LOADS[1:]:
            if (a, j) == (PASSES - 1, 1):
                nc.sync.dma_start(out=head_raw[:], in_=w[0:K_PASS, :].rearrange("(p j) n -> p j n", j=PACK))
            load_x(a, j, count)
        for m, a in parts:
            load_w(m, a)
            if a == PASSES - 1 and m in (1, 2):
                for d in (2 * m - 2, 2 * m - 1):
                    nc.sync.dma_start(neigh[d][:], (pos1, pos2, pos3, pos4)[d])

        make_identity(nc, ident[:])

        v_halves = [slice(h * P, (h + 1) * P) for h in range(V_HALVES)]
        woven = gates[:].rearrange("p d (q i) -> p (d q) i", i=RUN)
        for e in range(RUN // LINE):
            spread = psum.tile([P, LINE, P], F32, name=f"spread{e}", tag=f"back{e}")
            for i in range(LINE):
                column = gate_runs[:, e * LINE + i : e * LINE + i + 1]
                nc.tensor.transpose(spread[:, i, :], column.to_broadcast([P, P]), ident[:])
            nc.vector.tensor_copy(woven[:, :, e * LINE : (e + 1) * LINE], spread[:].rearrange("p i q -> p q i"))
        bias_turned = psum.tile([P, P], F32, name="bias_turned", tag="across")
        nc.tensor.transpose(bias_turned[:], bias_rows[:], ident[:])
        for m in range(BLOCKS):
            nc.vector.tensor_copy(bias_cols[m], bias_turned[:, m : m + 1])

        def gather(a, j, first, count, on_vector):
            window = x_raw[a, j].indirect(picked[:, first // LIST_ROWS : (first + count) // LIST_ROWS])
            if on_vector:
                nc.vector.tensor_copy(got[a][:, j, first : first + count], window)
            else:
                nc.scalar.activation(got[a][:, j, first : first + count], window, ACT.Copy)

        def weave(dst, src, on_vector):
            src = src.rearrange("p j (c i) -> p c j i", i=LINE)
            dst = dst.rearrange("p (c i) j -> p c j i", i=LINE)
            if on_vector:
                nc.vector.tensor_copy(dst, src)
            else:
                nc.scalar.activation(dst, src, ACT.Copy)

        def weave_x(a, first, end, on_vector):
            weave(x_bf[a][:, first:end, :], got[a][:, :, first:end], on_vector)

        def quantize_x(a, first, end):
            nc.vector.quantize_mx(
                out=x_words[a][:, first:end].bitcast(FP8X4),
                scales=x_bytes[a][:, first:end],
                in_=x_bf[a][:, first:end, :].rearrange("p t j -> p (t j)"),
            )

        def weights(m, a):
            if a == 0:
                return head_words[:, m * P : (m + 1) * P], head_bytes[:, m * P : (m + 1) * P]
            lo = max(lo for block, lo in CALLS if block == m and lo <= a)
            return w_words[m, lo][:, a - lo, :], w_bytes[m, lo][:, a - lo, :]

        def round_w(m, lo, on_vector=(), passes=None):
            hi = CALLS[m, lo]
            shape, name = [P, hi - lo, P, PACK], f"w_bf{m}_{lo}"
            if (m, lo) in w_bf:
                pass
            elif m < 2:
                w_bf[m, lo] = placed.tile(shape, BF16, name=name, offset=last_plane + (2 * m + lo - 1) * KIB, align_bytes=256)
            else:
                w_bf[m, lo] = keep.tile(shape, BF16, name=name, tag=f"bias{m - 2}", align_bytes=256)
            for a in passes or range(lo, hi):
                weave(w_bf[m, lo][:, a - lo, :, :], w_raw[m, a], a in on_vector)

        def quantize_w(m, lo):
            nc.vector.quantize_mx(
                out=w_words[m, lo][:].rearrange("p a n -> p (a n)").bitcast(FP8X4),
                scales=w_bytes[m, lo][:].rearrange("p a n -> p (a n)"),
                in_=w_bf[m, lo][:].rearrange("p a n j -> p (a n j)"),
            )

        def layer(m):
            groups = [slice(0, S)] if m in (1, 2) else [slice(0, S_HALF), slice(S_HALF, S)]
            accs = [psum.tile([P, cols.stop - cols.start], F32, name=f"acc{m}_{h}", tag=f"acc{m % 3}_{h}") for h, cols in enumerate(groups)]
            steps = [(a, h) for a in range(PASSES) for h in range(len(groups))]
            for a, h in steps if m == 0 else sorted(steps, key=lambda step: step[1]):
                words, scales = weights(m, a)
                nc.tensor.matmul_mx(
                    out=accs[h][:],
                    lhsT=words.bitcast(FP8X4),
                    lhsT_scale=scales,
                    rhs=x_words[a][:, groups[h]].bitcast(FP8X4),
                    rhs_scale=x_bytes[a][:, groups[h]],
                    start=(a == 0),
                    stop=(a == PASSES - 1),
                )
            if m == 2:
                y[m] = placed.tile([P, S], F32, name=f"y{m}", offset=slot[3, 1], align_bytes=256)
            elif m + 1 < BLOCKS:
                y[m] = placed.tile([P, S], F32, name=f"y{m}", offset=slot[m + 1, PASSES - 1] - KIB, align_bytes=256)
            else:
                y[m] = keep.tile([P, S], F32, name=f"y{m}", align_bytes=256)
            for h, cols in enumerate(groups):
                nc.scalar.activation(y[m][:, cols], accs[h][:], ACT.Identity, bias=bias_cols[m])

        def shifted(tile):
            return tile[:, SHIFT:].rearrange("p (i v) -> p i v", v=V)

        def term(m, d, dst):
            terms[m, d] = dst
            nc.vector.tensor_tensor(dst, y[m][:].indirect(neigh[d][:]), gates[:, d, :], ALU.mult)

        def store(m):
            nc.sync.dma_start(out=out[m * P : (m + 1) * P, :], in_=result[m])

        last_pass = PASSES - 1
        for a, j in planes:
            share = VECTOR_ENTRIES.get((a, j), 0)
            if share:
                gather(a, j, 0, share, True)
            if share < S:
                gather(a, j, share, S - share, False)
            if j == PACK - 1 and a < last_pass:
                weave_x(a, 0, S, True)
                quantize_x(a, 0, S)
            if (a, j) == (last_pass, 0):
                weave(head_bf[:, HEAD_SHARE:, :], head_raw[:, :, HEAD_SHARE:], False)
                weave(head_bf[:, :HEAD_SHARE, :], head_raw[:, :, :HEAD_SHARE], True)
                nc.vector.quantize_mx(out=head_words[:].bitcast(FP8X4), scales=head_bytes[:], in_=head_bf[:].rearrange("p n j -> p (n j)"))
        for h in range(2):
            weave_x(last_pass, h * S_HALF, (h + 1) * S_HALF, h == 0)
        round_w(0, 1, (1,))
        quantize_x(last_pass, 0, S_HALF)
        quantize_w(0, 1)
        quantize_x(last_pass, S_HALF, S)
        round_w(0, 2)
        quantize_w(0, 2)
        round_w(1, 1, (2,))
        layer(0)
        quantize_w(1, 1)

        def term_tile(count, name, offset=None):
            if offset is None:
                return shifted(keep.tile([P, count * V + SHIFT], F32, name=name, align_bytes=256))
            return shifted(placed.tile([P, count * V + SHIFT], F32, name=name, offset=offset, align_bytes=256))

        def across_halves(m, order, tags, held):
            banks = [psum.tile([P, P], F32, name=f"across{m}_{h}", tag=tag) for h, tag in enumerate(tags)]
            for i, d in enumerate(order):
                for h, cols in enumerate(v_halves):
                    nc.tensor.matmul(banks[h][:], terms[m, d][:, cols], ident[:], start=(i == 0), stop=(i == len(order) - 1), is_transpose=True)
            turned[m] = held
            for h, cols in enumerate(v_halves):
                nc.scalar.copy(held[:, cols], banks[h][:])

        def back(m, tag):
            bank = psum.tile([P, V], F32, name=f"back{m}", tag=tag)
            for cols in v_halves:
                nc.tensor.transpose(bank[:, cols], turned[m][:, cols], ident[:])
            return bank

        def fetch(m, d, dst):
            fetched[m, d] = dst
            nc.scalar.activation(dst, y[m][:].indirect(neigh[d][:]), ACT.Copy)

        def weigh(m, d, dst):
            terms[m, d] = dst
            nc.vector.tensor_tensor(dst, fetched[m, d], gates[:, d, :], ALU.mult)

        turned = {}
        free_terms = term_tile(2, "free_terms")
        round_w(2, 1)
        layer(1)
        for d in range(2):
            term(0, d, free_terms[:, d, :])
        quantize_w(2, 1)
        held_terms = term_tile(4, "held_terms", slot[2, 2] + KIB)
        for d in (2, 3):
            term(0, d, held_terms[:, d - 2, :])
        round_w(3, 1, (), (1,))
        layer(2)
        round_w(3, 1, (), (2,))
        for d in range(2):
            term(1, d, held_terms[:, 2 + d, :])
        quantize_w(3, 1)
        held_terms = term_tile(1, "later_terms", slot[3, 2] + KIB)
        term(1, 2, held_terms[:, 0, :])
        fetched = {}
        first_fetched = placed.tile([P, 2, V], F32, name="first_fetched", offset=slot[3, 2] - KIB, align_bytes=256)
        for d in range(2):
            fetch(2, d, first_fetched[:, d, :])
        layer(3)
        spare = shifted(keep.tile([P, (BLOCKS + 1) * V + SHIFT], F32, name="spare", tag="bias3", align_bytes=256))
        fetch(3, 0, spare[:, BLOCKS, :])
        last_terms = term_tile(2 * D - 1, "last_terms")
        weigh(2, 0, last_terms[:, D, :])
        term(2, 2, last_terms[:, D + 2, :])
        weigh(2, 1, last_terms[:, D + 1, :])
        for d in (1, 2):
            term(3, d, last_terms[:, d, :])
        weigh(3, 0, last_terms[:, 0, :])
        term(1, 3, gates[:, 1, :])
        term(2, 3, gates[:, 2, :])
        term(3, 3, last_terms[:, 3, :])

        early = psum.tile([P, 2, V], F32, name="early_across", tag="back1")
        for m in range(2):
            for cols in v_halves:
                for d in range(D - m):
                    nc.tensor.matmul(early[:, m, cols], terms[m, d][:, cols], ident[:], start=(d == 0), stop=(d == D - m - 1), is_transpose=True)
        nc.scalar.copy(spare[:, 0:2, :], early[:])
        across_halves(2, (0, 2, 1), ("acc2_0", "across"), spare[:, 2, :])
        early_back = psum.tile([P, 2, V], F32, name="early_back", tag="back0")
        for m in range(2):
            for cols in v_halves:
                nc.tensor.transpose(early_back[:, m, cols], spare[:, m, cols], ident[:])
        nc.scalar.copy(result[0], early_back[:, 0, :])
        store(0)
        across_halves(3, (1, 2, 0), ("acc0_0", "acc0_1"), spare[:, 3, :])
        banks = {1: early_back[:, 1, :], 2: back(2, "acc1_0")[:], 3: back(3, "eighth")[:]}
        for m in (1, 2, 3):
            nc.vector.tensor_tensor(result[m], banks[m], terms[m, D - 1], ALU.add)
            store(m)
